import numpy as np
import ml_dtypes


def mxq(x, axis, fmt="e4m3"):
    dtype, down = {"e4m3": (ml_dtypes.float8_e4m3fn, 7), "e5m2": (ml_dtypes.float8_e5m2, 14)}[fmt]
    v = np.moveaxis(np.asarray(x, np.float32).astype(ml_dtypes.bfloat16).astype(np.float64), axis, -1)
    blocks = v.reshape(v.shape[:-1] + (-1, 32))
    amax = np.abs(blocks).max(-1, keepdims=True)
    byte = np.maximum(np.where(amax > 0, np.frexp(amax)[1] - 1 + 127, 0) - down, 1)
    scale = np.exp2(byte - 127.0)
    codes = (blocks / scale).astype(np.float32).astype(dtype).astype(np.float64)
    return np.moveaxis((codes * scale).reshape(v.shape), -1, axis)


WIDE = False


def mx_kscale(k):
    if not WIDE:
        return np.ones(k)
    levels = np.array([10, -10, 5, -5, 0])
    if k % 512:
        return np.exp2(np.random.permutation(np.resize(levels, k // 32))).repeat(32)
    a = np.empty((k // 512, 16))
    for p in range(k // 512):
        a[p, :8] = np.random.permutation(np.resize(levels, 8))
        for g in range(8):
            far = levels[np.abs(levels - a[p, g]) >= 10]
            a[p, g + 8] = far[np.random.randint(len(far))]
    return np.exp2(a.ravel()).repeat(32)


BF16 = ml_dtypes.bfloat16


def bf(x):
    return np.asarray(x, np.float32).astype(BF16)


def f64(x):
    return np.asarray(x).astype(np.float64)


E2M1 = np.array([0.0, 0.5, 1.0, 1.5, 2.0, 3.0, 4.0, 6.0, -0.0, -0.5, -1.0, -1.5, -2.0, -3.0, -4.0, -6.0])


def pack_weight(w, fmt):
    k, n = w.shape
    w = f64(bf(w)).reshape(k // 32, 32, n)
    amax = np.abs(w).max(1)
    if fmt == "e4m3":
        byte = np.frexp(amax)[1] - 1 + 127 - 7
    else:
        mant, ex = np.frexp(amax / 6.0)
        byte = np.where(mant > 0.5, ex, ex - 1) + 127
    byte = np.clip(np.where(amax > 0, byte, 1), 1, 254)
    scaled = (w * np.exp2(127.0 - byte)[:, None, :]).reshape(k, n).astype(np.float32)
    by_word = np.ascontiguousarray(scaled.reshape(k // 512, 128, 4, n).transpose(0, 1, 3, 2))
    if fmt == "e4m3":
        words = by_word.astype(ml_dtypes.float8_e4m3fn).view(np.uint8)
    else:
        c = by_word.astype(ml_dtypes.float4_e2m1fn).view(np.uint8) & 0xF
        words = c[..., 0::2] | (c[..., 1::2] << 4)
    return np.ascontiguousarray(words), np.ascontiguousarray(byte.astype(np.uint8).reshape(k // 512, 16, n))


def unpack_weight(words, scales, fmt):
    g, p, n, _ = words.shape
    if fmt == "e4m3":
        vals = np.ascontiguousarray(words).view(ml_dtypes.float8_e4m3fn).astype(np.float64)
    else:
        nib = np.empty((g, p, n, 4), np.uint8)
        nib[..., 0::2] = words & 0xF
        nib[..., 1::2] = words >> 4
        vals = E2M1[nib]
    vals = vals * np.repeat(np.exp2(scales.astype(np.float64) - 127.0), 8, axis=1)[..., None]
    return vals.transpose(0, 1, 3, 2).reshape(g * 512, n)
def pack4(w):
    words, scales = pack_weight(w, "e2m1")
    return words.reshape(words.shape[0], 128, -1), scales


def unpack4(words, scales):
    return unpack_weight(words.reshape(words.shape[0], 128, -1, 2), scales, "e2m1")


M, K, V, T = 2048, 1024, 3072, 512


def draw0():
    s = mx_kscale(K)
    u = mx_kscale(M)
    z = np.random.standard_normal((M, V)) / np.sqrt(M) / u[:, None]
    geno_words, geno_scales = pack4(z)
    return {
        "pred": bf(np.random.standard_normal((M, K)) * s * u[:, None]),
        "eff": bf(np.random.standard_normal((K, T)) / np.sqrt(K) / s[:, None]),
        "traits": bf(np.random.standard_normal((M, T)) * u[:, None]),
        "geno_words": geno_words,
        "geno_scales": geno_scales,
        "var": bf(np.exp(0.3 * np.random.standard_normal(V))),
    }


def core(pred, eff, traits, geno_words, geno_scales, var):
    fit = mxq(f64(pred), 1, "e4m3") @ mxq(f64(eff), 0, "e4m3")
    resid = f64(traits) - fit
    z = unpack4(geno_words, geno_scales)
    score = z.T @ mxq(resid, 0, "e4m3")
    return np.square(score) / f64(var)[:, None]


def e4m3fn_bytes(y):
    return np.clip(np.asarray(y, np.float64), -448.0, 448.0).astype(np.float32).astype(ml_dtypes.float8_e4m3fn).view(np.uint8)


def e4m3fn_values(b):
    return np.asarray(b, np.uint8).view(ml_dtypes.float8_e4m3fn).astype(np.float64)


def setup_inputs():
    d = draw0()
    x0 = np.asarray(d['eff']).astype(np.float64)
    s = (np.max(np.abs(x0), axis=(1,), keepdims=True) / 448.0).astype(np.float32)
    out = {}
    for k, v in d.items():
        if k == 'eff':
            out['eff_bytes'] = e4m3fn_bytes(x0 / s.astype(np.float64))
            out['eff_scale'] = s
        else:
            out[k] = v
    return out


def reference(pred, eff_bytes, eff_scale, traits, geno_words, geno_scales, var):
    return core(pred, e4m3fn_values(eff_bytes) * eff_scale.astype(np.float64), traits, geno_words, geno_scales, var)

@@ -1,0 +1,398 @@
+from contextlib import ExitStack
+
+import concourse.mybir as mybir
+from concourse.masks import make_identity
+
+INDIV, PRED, VARIANTS, TRAITS = 2048, 1024, 3072, 512
+FLOPS = 2 * INDIV * PRED * TRAITS + 2 * INDIV * VARIANTS * TRAITS
+
+F32 = mybir.dt.float32
+BF16 = mybir.dt.bfloat16
+I32 = mybir.dt.int32
+U32 = mybir.dt.uint32
+U8 = mybir.dt.uint8
+FP8 = mybir.dt.float8_e4m3fn
+FP8X4 = mybir.dt.float8_e4m3fn_x4
+FP4X4 = mybir.dt.float4_e2m1fn_x4
+ACT = mybir.ActivationFunctionType
+ALU = mybir.AluOpType
+
+P = 128
+PACK = 4
+K_PASS = P * PACK
+G = INDIV // K_PASS
+H = PRED // K_PASS
+NV = VARIANTS // P
+HALF = TRAITS // 2
+W_CHUNKS = ((0, 6), (6, 12), (12, 18), (18, 24))
+
+
+def tile_gwas_score_statistics_s13_kernel(
+    tc, pred, eff_bytes, eff_scale, traits, geno_words, geno_scales, var, out
+):
+    nc = tc.nc
+    with ExitStack() as ctx:
+        keep = ctx.enter_context(tc.tile_pool(name="keep", bufs=1))
+        work = ctx.enter_context(tc.tile_pool(name="work", bufs=3))
+        psum = ctx.enter_context(tc.psum_pool(name="psum", bufs=2))
+        ctx.enter_context(tc.manual_schedule())
+
+        ident = keep.tile([P, P], F32, name="ident")
+        make_identity(nc, ident[:])
+        ident_b = keep.tile([P, P], BF16, name="ident_b")
+        make_identity(nc, ident_b[:])
+        var_rows = keep.tile([P, P], BF16, name="var_rows")
+        nc.gpsimd.memset(var_rows[:], 0.0)
+        zeros = keep.tile([P, TRAITS], BF16, name="zeros")
+        nc.vector.memset(zeros[:], 0.0)
+        one = keep.tile([P, 1], F32, name="one")
+        nc.vector.memset(one[:], 1.0)
+        g_scales = keep.tile([P, G * VARIANTS], U8, name="g_scales", align_bytes=64)
+        nc.vector.memset(g_scales[:].bitcast(I32), 0)
+
+        e_scale = keep.tile([P, H * PACK], F32, name="e_scale")
+        nc.scalar.dma_start(
+            out=e_scale[:].rearrange("p (h t) -> p h t", h=H),
+            in_=eff_scale.rearrange("(h p t) o -> p h (t o)", p=P, t=PACK),
+        )
+        root = keep.tile([P, 1], F32, name="root")
+        nc.scalar.activation(out=root[:], in_=one[:], func=ACT.Sqrt)
+
+        e_bytes = []
+        for h in range(H):
+            eb = keep.tile([P, PACK * TRAITS], U8, name="e_bytes%d" % h, align_bytes=64)
+            e_bytes.append(eb)
+
+        def load_eff(h):
+            nc.sync.dma_start(
+                out=e_bytes[h][:],
+                in_=eff_bytes.rearrange("(h p t) n -> h p (t n)", p=P, t=PACK)[h],
+            )
+
+        pred_v = pred.rearrange("(g p t) k -> g p t k", p=P, t=PACK)
+        traits_v = traits.rearrange("(g p t) n -> g p t n", p=P, t=PACK)
+        p_raw, t_raw = [], []
+        for g in range(G):
+            pr = keep.tile([P, PACK, PRED], BF16, name="p_raw%d" % g, align_bytes=64)
+            p_raw.append(pr)
+            tr = keep.tile([P, PACK, TRAITS], BF16, name="t_raw%d" % g, align_bytes=64)
+            t_raw.append(tr)
+
+        def load_pred(g, t0, t1):
+            nc.sync.dma_start(out=p_raw[g][:, t0:t1, :], in_=pred_v[g, :, t0:t1, :])
+
+        def load_traits(g):
+            nc.sync.dma_start(out=t_raw[g][:], in_=traits_v[g])
+
+        g_words = keep.tile([P, G, 2 * VARIANTS], U8, name="g_words", align_bytes=64)
+        words_v = geno_words.bitcast(I32)
+        words_flat = g_words[:].rearrange("p g n -> p (g n)").bitcast(I32)
+        words_sb = words_flat.rearrange("p (g n) -> p g n", g=G)
+        scales_v = geno_scales.bitcast(I32)
+        scales_sb = g_scales[:].bitcast(I32).rearrange("p (g n) -> p g n", g=G)
+
+        def load_words(v0, v1):
+            cols = slice(v0 * P // 2, v1 * P // 2)
+            nc.sync.dma_start(
+                out=words_sb[:, :, cols], in_=words_v[:, :, cols].rearrange("g p n -> p g n")
+            )
+
+        scale_rows = scales_v.rearrange("g (q r) n -> r q g n", r=4)
+
+        def load_scales(r):
+            nc.sync.dma_start(out=scales_sb[r : P : 32, :, :], in_=scale_rows[r])
+
+        load_pred(0, 0, 1)
+        load_eff(0)
+        load_eff(1)
+        load_pred(0, 1, 2)
+        load_pred(0, 2, 4)
+        load_pred(1, 0, 2)
+        load_traits(0)
+        load_pred(1, 2, 4)
+        load_pred(2, 0, 2)
+        load_pred(2, 2, 4)
+        load_traits(1)
+        nc.sync.dma_start(out=var_rows[0:NV, :], in_=var.rearrange("(j p) -> j p", p=P))
+        load_pred(3, 0, 2)
+        load_pred(3, 2, 4)
+        load_traits(2)
+        load_traits(3)
+        load_words(*W_CHUNKS[0])
+        for r in range(4):
+            load_scales(r)
+        for v0, v1 in W_CHUNKS[1:]:
+            load_words(v0, v1)
+
+        e_wide = keep.tile([P, H, PACK, TRAITS], BF16, name="e_wide", align_bytes=64)
+        e_grp = keep.tile([P, 2, H, HALF, PACK], BF16, name="e_grp", align_bytes=64)
+        e_codes = keep.tile([P, 2, H, HALF], U32, name="e_codes", align_bytes=64)
+        e_sc = keep.tile([P, 2, H, HALF], U8, name="e_sc", align_bytes=64)
+        p_codes, p_sc = [], []
+        for g in range(G):
+            pc = keep.tile([P, PACK, H, P], U32, name="p_codes%d" % g, align_bytes=64)
+            p_codes.append(pc)
+            ps = keep.tile([P, PACK, H, P], U8, name="p_sc%d" % g, align_bytes=64)
+            p_sc.append(ps)
+        r_codes = keep.tile([P, G, TRAITS], U32, name="r_codes", align_bytes=64)
+        r_sc = keep.tile([P, G, TRAITS], U8, name="r_sc", align_bytes=64)
+        rstd = keep.tile([P, NV], F32, name="rstd")
+        rvar = keep.tile([P, NV], F32, name="rvar")
+
+        def widen(h, t, on_vector=False):
+            raw = e_bytes[h][:, t * TRAITS : (t + 1) * TRAITS].bitcast(FP8)
+            scale = e_scale[:, h * PACK + t : h * PACK + t + 1]
+            if on_vector:
+                nc.vector.tensor_scalar(
+                    out=e_wide[:, h, t, :], in0=raw, scalar1=scale, scalar2=None, op0=ALU.mult
+                )
+            else:
+                nc.scalar.activation(out=e_wide[:, h, t, :], in_=raw, func=ACT.Copy, scale=scale)
+
+        def interleave(dst, src, on_vector):
+            dst = dst.rearrange("p (c i) t -> p c t i", i=4)
+            src = src.rearrange("p t (c i) -> p c t i", i=4)
+            if on_vector:
+                nc.vector.tensor_copy(out=dst, in_=src)
+            else:
+                nc.scalar.copy(out=dst, in_=src)
+
+        def inter_eff(nh, h, on_vector=False):
+            cols = slice(nh * HALF, (nh + 1) * HALF)
+            interleave(e_grp[:, nh, h, :, :], e_wide[:, h, :, cols], on_vector)
+
+        def quant_eff(nh):
+            nc.vector.quantize_mx(
+                out=e_codes[:, nh, :, :].rearrange("p h n -> p (h n)").bitcast(FP8X4),
+                scales=e_sc[:, nh, :, :].rearrange("p h n -> p (h n)"),
+                in_=e_grp[:, nh, :, :, :].rearrange("p h n t -> p (h n t)"),
+            )
+
+        p_grp, turned = {}, {}
+
+        def warm(n):
+            for i in range(n):
+                nc.tensor.matmul(
+                    warm_bank[:], lhsT=zeros[:, 0:P], rhs=zeros[:], start=True, stop=True
+                )
+
+        def turn(g, t):
+            bank = psum.tile([P, H, 2, P], F32, name="tp", bufs=3)
+            turned[g, t] = bank
+            words = p_raw[g][:, t, :].bitcast(F32)
+            for h in range(H):
+                for u in range(2):
+                    src = words[:, 256 * h + u : 256 * (h + 1) : 2]
+                    nc.tensor.transpose(bank[:, h, u, :], src, ident[:])
+
+        def take(g, t, on_vector=False):
+            if g not in p_grp:
+                pg = work.tile([P, PACK, H, P, PACK], BF16, name="p_grp", bufs=2, align_bytes=64)
+                p_grp[g] = pg
+            dst = p_grp[g][:, t, :, :, :].rearrange("p h r j -> p (h r j)").bitcast(F32)
+            dst = dst.rearrange("p (h r u) -> p h r u", h=H, u=2)
+            src = turned[g, t][:].rearrange("p h u r -> p h r u")
+            if on_vector:
+                nc.vector.tensor_copy(out=dst, in_=src)
+            else:
+                nc.scalar.copy(out=dst, in_=src)
+
+        def quant_pred(g, t0, t1):
+            nc.vector.quantize_mx(
+                out=p_codes[g][:, t0:t1, :, :].rearrange("p t h r -> p (t h r)").bitcast(FP8X4),
+                scales=p_sc[g][:, t0:t1, :, :].rearrange("p t h r -> p (t h r)"),
+                in_=p_grp[g][:, t0:t1, :, :, :].rearrange("p t h r j -> p (t h r j)"),
+            )
+
+        fit_bank, r_plain, r_grp = {}, {}, {}
+
+        def fit(g, t, nhs=None):
+            if (g, t) not in fit_bank:
+                bank = psum.tile([P, TRAITS], F32, name="fit", bufs=3)
+                fit_bank[g, t] = bank
+            for nh in range(2) if nhs is None else nhs:
+                for h in range(H):
+                    nc.tensor.matmul_mx(
+                        out=fit_bank[g, t][:, nh * HALF : (nh + 1) * HALF],
+                        lhsT=p_codes[g][:, t, h, :].bitcast(FP8X4),
+                        lhsT_scale=p_sc[g][:, t, h, :],
+                        rhs=e_codes[:, nh, h, :].bitcast(FP8X4),
+                        rhs_scale=e_sc[:, nh, h, :],
+                        start=(h == 0),
+                        stop=(h == H - 1),
+                    )
+
+        def resid(g, t):
+            if g not in r_plain:
+                rp = work.tile([P, PACK, TRAITS], BF16, name="r_plain", bufs=3)
+                r_plain[g] = rp
+            nc.vector.tensor_tensor(
+                out=r_plain[g][:, t, :], in0=t_raw[g][:, t, :], in1=fit_bank[g, t][:], op=ALU.subtract
+            )
+
+        def inter_resid(g, a, on_vector=False):
+            if g not in r_grp:
+                rg = work.tile([P, TRAITS, PACK], BF16, name="r_grp", bufs=3, align_bytes=64)
+                r_grp[g] = rg
+            cols = slice(a * HALF, (a + 1) * HALF)
+            interleave(r_grp[g][:, cols, :], r_plain[g][:, :, cols], on_vector)
+
+        def quant_resid(g, a0, a1):
+            cols = slice(a0 * HALF, a1 * HALF)
+            nc.vector.quantize_mx(
+                out=r_codes[:, g, cols].bitcast(FP8X4),
+                scales=r_sc[:, g, cols],
+                in_=r_grp[g][:, cols, :].rearrange("p n t -> p (n t)"),
+            )
+
+        score_bank = {}
+        bank_names = ("sc", "sc", "tp", "tp", "tp", "fit", "fit", "fit")
+        bank_bufs = {"sc": 2, "tp": 3, "fit": 3}
+
+        def score(v, g):
+            if g == 0:
+                which = bank_names[v % len(bank_names)]
+                bank = psum.tile([P, TRAITS], F32, name=which, bufs=bank_bufs[which])
+                score_bank[v] = bank
+            nc.tensor.matmul_mx(
+                out=score_bank[v][:],
+                lhsT=g_words[:, g, 2 * v * P : 2 * (v + 1) * P].bitcast(FP4X4),
+                lhsT_scale=g_scales[:, g * VARIANTS + v * P : g * VARIANTS + (v + 1) * P],
+                rhs=r_codes[:, g, :].bitcast(FP8X4),
+                rhs_scale=r_sc[:, g, :],
+                start=(g == 0),
+                stop=(g == G - 1),
+            )
+
+        def finish(v):
+            res = work.tile([P, TRAITS], F32, name="res", bufs=6)
+            parts = 2 if v == NV - 1 else 1
+            width = TRAITS // parts
+            for i in range(parts):
+                cols = slice(i * width, (i + 1) * width)
+                nc.scalar.activation(
+                    out=res[:, cols],
+                    in_=score_bank[v][:, cols],
+                    func=ACT.Square,
+                    scale=rstd[:, v : v + 1],
+                )
+                nc.sync.dma_start(out=out[v * P : (v + 1) * P, cols], in_=res[:, cols])
+
+        warm_bank = psum.tile([P, TRAITS], F32, name="sc", bufs=2)
+        warm(5)
+        turn(0, 0)
+        widen(0, 0, True)
+        widen(0, 1)
+        warm(1)
+        widen(0, 3, True)
+        take(0, 0)
+        widen(1, 1, True)
+        warm(1)
+        widen(1, 2, True)
+        widen(1, 3)
+        turn(0, 1)
+        widen(0, 2, True)
+        widen(1, 0, True)
+        turn(0, 2)
+        inter_eff(0, 0, True)
+        take(0, 1)
+        turn(0, 3)
+        inter_eff(0, 1)
+        take(0, 2, True)
+        turn(1, 0)
+        quant_pred(0, 0, 2)
+        inter_eff(1, 1)
+        turn(1, 1)
+        quant_eff(0)
+        take(0, 3)
+        inter_eff(1, 0, True)
+        fit(0, 0, (0,))
+        fit(0, 1, (0,))
+        quant_eff(1)
+        take(1, 0)
+        take(1, 1)
+        turn(1, 2)
+        quant_pred(0, 2, 4)
+        turn(1, 3)
+        take(1, 2, True)
+        fit(0, 0, (1,))
+        fit(0, 1, (1,))
+        take(1, 3)
+        turn(2, 0)
+        resid(0, 0)
+        turn(2, 1)
+        resid(0, 1)
+        take(2, 0)
+        fit(0, 2)
+        quant_pred(1, 0, 4)
+        take(2, 1)
+        fit(0, 3)
+        turn(2, 2)
+        resid(0, 2)
+        turn(2, 3)
+        take(2, 2)
+        fit(1, 0)
+        resid(0, 3)
+        take(2, 3)
+        fit(1, 1)
+        resid(1, 0)
+        inter_resid(0, 0)
+        turn(3, 0)
+        quant_pred(2, 0, 4)
+        fit(1, 2)
+        inter_resid(0, 1)
+        turn(3, 1)
+        turn(3, 2)
+        resid(1, 1)
+        take(3, 0)
+        fit(2, 0)
+        resid(1, 2)
+        take(3, 1)
+        fit(2, 1)
+        quant_resid(0, 0, 2)
+        take(3, 2)
+        turn(3, 3)
+        var_bank = psum.tile([P, P], BF16, name="tp", bufs=3)
+        nc.tensor.transpose(var_bank[:], var_rows[:], ident_b[:])
+        resid(2, 0)
+        fit(1, 3)
+        take(3, 3)
+        resid(2, 1)
+        fit(2, 2)
+        resid(1, 3)
+        fit(2, 3)
+        quant_pred(3, 0, 4)
+        nc.vector.reciprocal(out=rvar[:], in_=var_bank[:, 0:NV])
+        nc.scalar.activation(out=rstd[:], in_=rvar[:], func=ACT.Sqrt)
+        inter_resid(1, 0)
+        inter_resid(1, 1)
+        resid(2, 2)
+        fit(3, 0)
+        resid(2, 3)
+        fit(3, 1)
+        resid(3, 0)
+        fit(3, 2)
+        inter_resid(2, 0)
+        quant_resid(1, 0, 2)
+        fit(3, 3)
+        inter_resid(2, 1)
+        resid(3, 1)
+        resid(3, 2)
+        resid(3, 3)
+        quant_resid(2, 0, 2)
+        inter_resid(3, 0)
+        inter_resid(3, 1, True)
+        quant_resid(3, 1, 2)
+        quant_resid(3, 0, 1)
+        for v in range(8):
+            score(v, 0)
+            score(v, 1)
+        for v in range(8):
+            score(v, 2)
+        for v in range(8):
+            score(v, 3)
+            finish(v)
+        for v in range(8, NV):
+            for g in range(G):
+                score(v, g)
+            finish(v)

@@ -43,8 +43,6 @@ def tile_gwas_score_statistics_s13_kernel(
         make_identity(nc, ident_b[:])
         var_rows = keep.tile([P, P], BF16, name="var_rows")
         nc.gpsimd.memset(var_rows[:], 0.0)
-        zeros = keep.tile([P, TRAITS], BF16, name="zeros")
-        nc.vector.memset(zeros[:], 0.0)
         one = keep.tile([P, 1], F32, name="one")
         nc.vector.memset(one[:], 1.0)
         g_scales = keep.tile([P, G * VARIANTS], U8, name="g_scales", align_bytes=64)
@@ -170,12 +168,6 @@ def tile_gwas_score_statistics_s13_kernel(
 
         p_grp, turned = {}, {}
 
-        def warm(n):
-            for i in range(n):
-                nc.tensor.matmul(
-                    warm_bank[:], lhsT=zeros[:, 0:P], rhs=zeros[:], start=True, stop=True
-                )
-
         def turn(g, t):
             bank = psum.tile([P, H, 2, P], F32, name="tp", bufs=3)
             turned[g, t] = bank
@@ -278,16 +270,12 @@ def tile_gwas_score_statistics_s13_kernel(
                 )
                 nc.sync.dma_start(out=out[v * P : (v + 1) * P, cols], in_=res[:, cols])
 
-        warm_bank = psum.tile([P, TRAITS], F32, name="sc", bufs=2)
-        warm(5)
         turn(0, 0)
         widen(0, 0, True)
         widen(0, 1)
-        warm(1)
         widen(0, 3, True)
         take(0, 0)
         widen(1, 1, True)
-        warm(1)
         widen(1, 2, True)
         widen(1, 3)
         turn(0, 1)

@@ -24,7 +24,8 @@ G = INDIV // K_PASS
 H = PRED // K_PASS
 NV = VARIANTS // P
 HALF = TRAITS // 2
-W_CHUNKS = ((0, 6), (6, 12), (12, 18), (18, 24))
+BANKS = 8
+QUAD = 32
 
 
 def tile_gwas_score_statistics_s13_kernel(
@@ -33,35 +34,40 @@ def tile_gwas_score_statistics_s13_kernel(
     nc = tc.nc
     with ExitStack() as ctx:
         keep = ctx.enter_context(tc.tile_pool(name="keep", bufs=1))
-        work = ctx.enter_context(tc.tile_pool(name="work", bufs=3))
-        psum = ctx.enter_context(tc.psum_pool(name="psum", bufs=2))
+        work = ctx.enter_context(tc.tile_pool(name="work", bufs=6))
+        psum = ctx.enter_context(tc.psum_pool(name="psum", bufs=1))
         ctx.enter_context(tc.manual_schedule())
 
-        ident = keep.tile([P, P], F32, name="ident")
-        make_identity(nc, ident[:])
-        ident_b = keep.tile([P, P], BF16, name="ident_b")
-        make_identity(nc, ident_b[:])
-        var_rows = keep.tile([P, P], BF16, name="var_rows")
-        nc.gpsimd.memset(var_rows[:], 0.0)
-        one = keep.tile([P, 1], F32, name="one")
-        nc.vector.memset(one[:], 1.0)
-        g_scales = keep.tile([P, G * VARIANTS], U8, name="g_scales", align_bytes=64)
-        nc.vector.memset(g_scales[:].bitcast(I32), 0)
+        def kept(shape, dtype, name):
+            return keep.tile(shape, dtype, name=name, align_bytes=64)
 
-        e_scale = keep.tile([P, H * PACK], F32, name="e_scale")
+        def bank(b):
+            return psum.tile([P, TRAITS], F32, name="bank%d" % b)
+
+        ident = kept([P, P], F32, "ident")
+        make_identity(nc, ident[:])
+        var_rows = kept([P, P], BF16, "var_rows")
+        nc.vector.memset(var_rows[0 : P - NV, :], 0.0)
+        scale_parts = ((0, BANKS), (BANKS, NV))
+        g_scales = []
+        for v0, v1 in scale_parts:
+            gs = kept([P, G, (v1 - v0) * P], U8, "g_scales%d" % v0)
+            nc.vector.memset(gs[:].rearrange("p g n -> p (g n)").bitcast(I32), 0)
+            g_scales.append(gs)
+
+        e_scale = kept([P, H * PACK], F32, "e_scale")
         nc.scalar.dma_start(
             out=e_scale[:].rearrange("p (h t) -> p h t", h=H),
             in_=eff_scale.rearrange("(h p t) o -> p h (t o)", p=P, t=PACK),
         )
-        root = keep.tile([P, 1], F32, name="root")
-        nc.scalar.activation(out=root[:], in_=one[:], func=ACT.Sqrt)
 
-        e_bytes = []
-        for h in range(H):
-            eb = keep.tile([P, PACK * TRAITS], U8, name="e_bytes%d" % h, align_bytes=64)
-            e_bytes.append(eb)
+        def load_var():
+            nc.sync.dma_start(out=var_rows[P - NV : P, :], in_=var.rearrange("(j p) -> j p", p=P))
+
+        e_bytes, p_raw, t_raw, g_words = {}, {}, {}, {}
 
         def load_eff(h):
+            e_bytes[h] = kept([P, PACK * TRAITS], U8, "e_bytes%d" % h)
             nc.sync.dma_start(
                 out=e_bytes[h][:],
                 in_=eff_bytes.rearrange("(h p t) n -> h p (t n)", p=P, t=PACK)[h],
@@ -69,312 +75,280 @@ def tile_gwas_score_statistics_s13_kernel(
 
         pred_v = pred.rearrange("(g p t) k -> g p t k", p=P, t=PACK)
         traits_v = traits.rearrange("(g p t) n -> g p t n", p=P, t=PACK)
-        p_raw, t_raw = [], []
-        for g in range(G):
-            pr = keep.tile([P, PACK, PRED], BF16, name="p_raw%d" % g, align_bytes=64)
-            p_raw.append(pr)
-            tr = keep.tile([P, PACK, TRAITS], BF16, name="t_raw%d" % g, align_bytes=64)
-            t_raw.append(tr)
 
         def load_pred(g, t0, t1):
-            nc.sync.dma_start(out=p_raw[g][:, t0:t1, :], in_=pred_v[g, :, t0:t1, :])
+            raw = kept([P, t1 - t0, PRED], BF16, "p_raw%d_%d" % (g, t0))
+            nc.sync.dma_start(out=raw[:], in_=pred_v[g, :, t0:t1, :])
+            for t in range(t0, t1):
+                p_raw[g, t] = raw[:, t - t0, :]
 
         def load_traits(g):
+            t_raw[g] = kept([P, PACK, TRAITS], BF16, "t_raw%d" % g)
             nc.sync.dma_start(out=t_raw[g][:], in_=traits_v[g])
 
-        g_words = keep.tile([P, G, 2 * VARIANTS], U8, name="g_words", align_bytes=64)
-        words_v = geno_words.bitcast(I32)
-        words_flat = g_words[:].rearrange("p g n -> p (g n)").bitcast(I32)
-        words_sb = words_flat.rearrange("p (g n) -> p g n", g=G)
-        scales_v = geno_scales.bitcast(I32)
-        scales_sb = g_scales[:].bitcast(I32).rearrange("p (g n) -> p g n", g=G)
+        words_v = geno_words.bitcast(I32).rearrange("g p n -> p g n")
 
-        def load_words(v0, v1):
-            cols = slice(v0 * P // 2, v1 * P // 2)
-            nc.sync.dma_start(
-                out=words_sb[:, :, cols], in_=words_v[:, :, cols].rearrange("g p n -> p g n")
-            )
+        def load_words(v0, v1, g0, g1):
+            words = kept([P, g1 - g0, (v1 - v0) * P // 2], I32, "g_words%d_%d" % (v0, g0))
+            nc.sync.dma_start(out=words[:], in_=words_v[:, g0:g1, v0 * P // 2 : v1 * P // 2])
+            for v in range(v0, v1):
+                for g in range(g0, g1):
+                    g_words[v, g] = words[:, g - g0, (v - v0) * P // 2 : (v - v0 + 1) * P // 2]
 
-        scale_rows = scales_v.rearrange("g (q r) n -> r q g n", r=4)
+        scale_rows = geno_scales.bitcast(I32).rearrange("g (q r) n -> r q g n", r=4)
 
-        def load_scales(r):
-            nc.sync.dma_start(out=scales_sb[r : P : 32, :, :], in_=scale_rows[r])
+        def load_scales(part):
+            v0, v1 = scale_parts[part]
+            dst = g_scales[part][:].rearrange("p g n -> p (g n)").bitcast(I32)
+            dst = dst.rearrange("p (g n) -> p g n", g=G)
+            for r in range(4):
+                nc.sync.dma_start(
+                    out=dst[r:P:QUAD, :, :], in_=scale_rows[r][:, :, v0 * P // 4 : v1 * P // 4]
+                )
 
-        load_pred(0, 0, 1)
-        load_eff(0)
-        load_eff(1)
-        load_pred(0, 1, 2)
-        load_pred(0, 2, 4)
-        load_pred(1, 0, 2)
-        load_traits(0)
-        load_pred(1, 2, 4)
-        load_pred(2, 0, 2)
-        load_pred(2, 2, 4)
-        load_traits(1)
-        nc.sync.dma_start(out=var_rows[0:NV, :], in_=var.rearrange("(j p) -> j p", p=P))
-        load_pred(3, 0, 2)
-        load_pred(3, 2, 4)
-        load_traits(2)
-        load_traits(3)
-        load_words(*W_CHUNKS[0])
-        for r in range(4):
-            load_scales(r)
-        for v0, v1 in W_CHUNKS[1:]:
-            load_words(v0, v1)
-
-        e_wide = keep.tile([P, H, PACK, TRAITS], BF16, name="e_wide", align_bytes=64)
-        e_grp = keep.tile([P, 2, H, HALF, PACK], BF16, name="e_grp", align_bytes=64)
-        e_codes = keep.tile([P, 2, H, HALF], U32, name="e_codes", align_bytes=64)
-        e_sc = keep.tile([P, 2, H, HALF], U8, name="e_sc", align_bytes=64)
-        p_codes, p_sc = [], []
+        e_wide, e_grp, e_codes, e_sc = {}, {}, {}, {}
+        for h in range(H):
+            e_wide[h] = kept([P, PACK, TRAITS], BF16, "e_wide%d" % h)
+            e_grp[h] = kept([P, TRAITS, PACK], BF16, "e_grp%d" % h)
+            e_codes[h] = kept([P, TRAITS], U32, "e_codes%d" % h)
+            e_sc[h] = kept([P, TRAITS], U8, "e_sc%d" % h)
+        p_grp, p_codes, p_sc = {}, {}, {}
+        r_plain, r_grp, r_codes, r_sc = {}, {}, {}, {}
         for g in range(G):
-            pc = keep.tile([P, PACK, H, P], U32, name="p_codes%d" % g, align_bytes=64)
-            p_codes.append(pc)
-            ps = keep.tile([P, PACK, H, P], U8, name="p_sc%d" % g, align_bytes=64)
-            p_sc.append(ps)
-        r_codes = keep.tile([P, G, TRAITS], U32, name="r_codes", align_bytes=64)
-        r_sc = keep.tile([P, G, TRAITS], U8, name="r_sc", align_bytes=64)
-        rstd = keep.tile([P, NV], F32, name="rstd")
-        rvar = keep.tile([P, NV], F32, name="rvar")
+            for a in range(2):
+                p_grp[g, a] = kept([P, 2, H, P, PACK], BF16, "p_grp%d_%d" % (g, a))
+                p_codes[g, a] = kept([P, 2, H, P], U32, "p_codes%d_%d" % (g, a))
+                p_sc[g, a] = kept([P, 2, H, P], U8, "p_sc%d_%d" % (g, a))
+            r_plain[g] = kept([P, PACK, TRAITS], BF16, "r_plain%d" % g)
+            r_grp[g] = kept([P, TRAITS, PACK], BF16, "r_grp%d" % g)
+            r_codes[g] = kept([P, TRAITS], U32, "r_codes%d" % g)
+            r_sc[g] = kept([P, TRAITS], U8, "r_sc%d" % g)
+        sd_rows = kept([P, P], F32, "sd_rows")
+        rstd = kept([P, NV], F32, "rstd")
+
+        def copy(dst, src, on_vector):
+            if on_vector:
+                nc.vector.tensor_copy(out=dst, in_=src)
+            else:
+                nc.scalar.copy(out=dst, in_=src)
+
+        def root_var():
+            nc.scalar.activation(out=sd_rows[:], in_=var_rows[:], func=ACT.Sqrt)
+
+        def turn_var(b):
+            turned["var"] = bank(b)
+            nc.tensor.transpose(turned["var"][:, 0:P], sd_rows[:], ident[:])
+
+        def take_var():
+            nc.vector.reciprocal(out=rstd[:], in_=turned["var"][:, P - NV : P])
 
         def widen(h, t, on_vector=False):
             raw = e_bytes[h][:, t * TRAITS : (t + 1) * TRAITS].bitcast(FP8)
             scale = e_scale[:, h * PACK + t : h * PACK + t + 1]
             if on_vector:
                 nc.vector.tensor_scalar(
-                    out=e_wide[:, h, t, :], in0=raw, scalar1=scale, scalar2=None, op0=ALU.mult
+                    out=e_wide[h][:, t, :], in0=raw, scalar1=scale, scalar2=None, op0=ALU.mult
                 )
             else:
-                nc.scalar.activation(out=e_wide[:, h, t, :], in_=raw, func=ACT.Copy, scale=scale)
+                nc.scalar.activation(out=e_wide[h][:, t, :], in_=raw, func=ACT.Copy, scale=scale)
 
         def interleave(dst, src, on_vector):
             dst = dst.rearrange("p (c i) t -> p c t i", i=4)
             src = src.rearrange("p t (c i) -> p c t i", i=4)
-            if on_vector:
-                nc.vector.tensor_copy(out=dst, in_=src)
-            else:
-                nc.scalar.copy(out=dst, in_=src)
+            copy(dst, src, on_vector)
 
-        def inter_eff(nh, h, on_vector=False):
-            cols = slice(nh * HALF, (nh + 1) * HALF)
-            interleave(e_grp[:, nh, h, :, :], e_wide[:, h, :, cols], on_vector)
+        def inter_eff(h, on_vector=False):
+            interleave(e_grp[h][:], e_wide[h][:], on_vector)
 
-        def quant_eff(nh):
+        def quant_eff(h):
             nc.vector.quantize_mx(
-                out=e_codes[:, nh, :, :].rearrange("p h n -> p (h n)").bitcast(FP8X4),
-                scales=e_sc[:, nh, :, :].rearrange("p h n -> p (h n)"),
-                in_=e_grp[:, nh, :, :, :].rearrange("p h n t -> p (h n t)"),
+                out=e_codes[h][:].bitcast(FP8X4),
+                scales=e_sc[h][:],
+                in_=e_grp[h][:].rearrange("p n t -> p (n t)"),
             )
 
-        p_grp, turned = {}, {}
+        turned, fitted, scored = {}, {}, {}
 
-        def turn(g, t):
-            bank = psum.tile([P, H, 2, P], F32, name="tp", bufs=3)
-            turned[g, t] = bank
-            words = p_raw[g][:, t, :].bitcast(F32)
+        def turn(g, t, b):
+            turned[g, t] = bank(b)[:].rearrange("p (h u r) -> p h u r", h=H, u=2)
+            words = p_raw[g, t].bitcast(F32)
             for h in range(H):
                 for u in range(2):
                     src = words[:, 256 * h + u : 256 * (h + 1) : 2]
-                    nc.tensor.transpose(bank[:, h, u, :], src, ident[:])
+                    nc.tensor.transpose(turned[g, t][:, h, u, :], src, ident[:])
 
         def take(g, t, on_vector=False):
-            if g not in p_grp:
-                pg = work.tile([P, PACK, H, P, PACK], BF16, name="p_grp", bufs=2, align_bytes=64)
-                p_grp[g] = pg
-            dst = p_grp[g][:, t, :, :, :].rearrange("p h r j -> p (h r j)").bitcast(F32)
+            dst = p_grp[g, t // 2][:, t % 2, :, :, :].rearrange("p h r j -> p (h r j)").bitcast(F32)
             dst = dst.rearrange("p (h r u) -> p h r u", h=H, u=2)
-            src = turned[g, t][:].rearrange("p h u r -> p h r u")
-            if on_vector:
-                nc.vector.tensor_copy(out=dst, in_=src)
-            else:
-                nc.scalar.copy(out=dst, in_=src)
+            copy(dst, turned[g, t].rearrange("p h u r -> p h r u"), on_vector)
 
-        def quant_pred(g, t0, t1):
+        def quant_pred(g, a):
             nc.vector.quantize_mx(
-                out=p_codes[g][:, t0:t1, :, :].rearrange("p t h r -> p (t h r)").bitcast(FP8X4),
-                scales=p_sc[g][:, t0:t1, :, :].rearrange("p t h r -> p (t h r)"),
-                in_=p_grp[g][:, t0:t1, :, :, :].rearrange("p t h r j -> p (t h r j)"),
+                out=p_codes[g, a][:].rearrange("p t h r -> p (t h r)").bitcast(FP8X4),
+                scales=p_sc[g, a][:].rearrange("p t h r -> p (t h r)"),
+                in_=p_grp[g, a][:].rearrange("p t h r j -> p (t h r j)"),
             )
 
-        fit_bank, r_plain, r_grp = {}, {}, {}
-
-        def fit(g, t, nhs=None):
-            if (g, t) not in fit_bank:
-                bank = psum.tile([P, TRAITS], F32, name="fit", bufs=3)
-                fit_bank[g, t] = bank
-            for nh in range(2) if nhs is None else nhs:
-                for h in range(H):
-                    nc.tensor.matmul_mx(
-                        out=fit_bank[g, t][:, nh * HALF : (nh + 1) * HALF],
-                        lhsT=p_codes[g][:, t, h, :].bitcast(FP8X4),
-                        lhsT_scale=p_sc[g][:, t, h, :],
-                        rhs=e_codes[:, nh, h, :].bitcast(FP8X4),
-                        rhs_scale=e_sc[:, nh, h, :],
-                        start=(h == 0),
-                        stop=(h == H - 1),
-                    )
+        def fit(g, t, b):
+            fitted[g, t] = bank(b)
+            for h in range(H):
+                nc.tensor.matmul_mx(
+                    out=fitted[g, t][:],
+                    lhsT=p_codes[g, t // 2][:, t % 2, h, :].bitcast(FP8X4),
+                    lhsT_scale=p_sc[g, t // 2][:, t % 2, h, :],
+                    rhs=e_codes[h][:].bitcast(FP8X4),
+                    rhs_scale=e_sc[h][:],
+                    start=(h == 0),
+                    stop=(h == H - 1),
+                )
 
         def resid(g, t):
-            if g not in r_plain:
-                rp = work.tile([P, PACK, TRAITS], BF16, name="r_plain", bufs=3)
-                r_plain[g] = rp
             nc.vector.tensor_tensor(
-                out=r_plain[g][:, t, :], in0=t_raw[g][:, t, :], in1=fit_bank[g, t][:], op=ALU.subtract
+                out=r_plain[g][:, t, :], in0=t_raw[g][:, t, :], in1=fitted[g, t][:], op=ALU.subtract
             )
 
         def inter_resid(g, a, on_vector=False):
-            if g not in r_grp:
-                rg = work.tile([P, TRAITS, PACK], BF16, name="r_grp", bufs=3, align_bytes=64)
-                r_grp[g] = rg
             cols = slice(a * HALF, (a + 1) * HALF)
             interleave(r_grp[g][:, cols, :], r_plain[g][:, :, cols], on_vector)
 
         def quant_resid(g, a0, a1):
             cols = slice(a0 * HALF, a1 * HALF)
             nc.vector.quantize_mx(
-                out=r_codes[:, g, cols].bitcast(FP8X4),
-                scales=r_sc[:, g, cols],
+                out=r_codes[g][:, cols].bitcast(FP8X4),
+                scales=r_sc[g][:, cols],
                 in_=r_grp[g][:, cols, :].rearrange("p n t -> p (n t)"),
             )
 
-        score_bank = {}
-        bank_names = ("sc", "sc", "tp", "tp", "tp", "fit", "fit", "fit")
-        bank_bufs = {"sc": 2, "tp": 3, "fit": 3}
-
         def score(v, g):
             if g == 0:
-                which = bank_names[v % len(bank_names)]
-                bank = psum.tile([P, TRAITS], F32, name=which, bufs=bank_bufs[which])
-                score_bank[v] = bank
+                scored[v] = bank(v % BANKS)
+            part = 0 if v < BANKS else 1
+            col = (v - scale_parts[part][0]) * P
             nc.tensor.matmul_mx(
-                out=score_bank[v][:],
-                lhsT=g_words[:, g, 2 * v * P : 2 * (v + 1) * P].bitcast(FP4X4),
-                lhsT_scale=g_scales[:, g * VARIANTS + v * P : g * VARIANTS + (v + 1) * P],
-                rhs=r_codes[:, g, :].bitcast(FP8X4),
-                rhs_scale=r_sc[:, g, :],
+                out=scored[v][:],
+                lhsT=g_words[v, g].bitcast(FP4X4),
+                lhsT_scale=g_scales[part][:, g, col : col + P],
+                rhs=r_codes[g][:].bitcast(FP8X4),
+                rhs_scale=r_sc[g][:],
                 start=(g == 0),
                 stop=(g == G - 1),
             )
 
         def finish(v):
-            res = work.tile([P, TRAITS], F32, name="res", bufs=6)
+            res = work.tile([P, TRAITS], F32, name="res")
             parts = 2 if v == NV - 1 else 1
             width = TRAITS // parts
             for i in range(parts):
                 cols = slice(i * width, (i + 1) * width)
                 nc.scalar.activation(
                     out=res[:, cols],
-                    in_=score_bank[v][:, cols],
+                    in_=scored[v][:, cols],
                     func=ACT.Square,
                     scale=rstd[:, v : v + 1],
                 )
                 nc.sync.dma_start(out=out[v * P : (v + 1) * P, cols], in_=res[:, cols])
 
-        turn(0, 0)
-        widen(0, 0, True)
-        widen(0, 1)
-        widen(0, 3, True)
+        load_eff(0)
+        load_pred(0, 0, 1)
+        load_eff(1)
+        load_pred(0, 1, 2)
+        load_pred(0, 2, 4)
+        load_pred(1, 0, 2)
+        load_pred(1, 2, 4)
+        load_var()
+        load_traits(0)
+        load_pred(2, 0, 2)
+        load_pred(2, 2, 4)
+        load_pred(3, 0, 2)
+        load_pred(3, 2, 4)
+        load_traits(1)
+        load_traits(2)
+        load_scales(0)
+        load_words(0, 8, 0, 2)
+        load_traits(3)
+        load_words(0, 8, 2, 4)
+        load_scales(1)
+        load_words(8, 16, 0, 4)
+        load_words(16, 24, 0, 4)
+
+        for t in range(4):
+            turn(0, t, t)
+        for t in range(4):
+            turn(1, t, 4 + t)
+        widen(0, 0)
+        for t in range(1, 4):
+            widen(0, t, True)
+        inter_eff(0, True)
         take(0, 0)
-        widen(1, 1, True)
-        widen(1, 2, True)
-        widen(1, 3)
-        turn(0, 1)
-        widen(0, 2, True)
-        widen(1, 0, True)
-        turn(0, 2)
-        inter_eff(0, 0, True)
+        widen(1, 0)
         take(0, 1)
-        turn(0, 3)
-        inter_eff(0, 1)
-        take(0, 2, True)
-        turn(1, 0)
-        quant_pred(0, 0, 2)
-        inter_eff(1, 1)
-        turn(1, 1)
+        widen(1, 1)
+        widen(1, 2, True)
+        widen(1, 3, True)
         quant_eff(0)
+        take(0, 2)
         take(0, 3)
-        inter_eff(1, 0, True)
-        fit(0, 0, (0,))
-        fit(0, 1, (0,))
+        inter_eff(1, True)
+        quant_pred(0, 0)
         quant_eff(1)
-        take(1, 0)
-        take(1, 1)
-        turn(1, 2)
-        quant_pred(0, 2, 4)
-        turn(1, 3)
-        take(1, 2, True)
-        fit(0, 0, (1,))
-        fit(0, 1, (1,))
-        take(1, 3)
-        turn(2, 0)
+        quant_pred(0, 1)
+        for t in range(4):
+            take(1, t)
+        for t in range(4):
+            fit(0, t, t)
+        root_var()
+        for t in range(4):
+            turn(2, t, 4 + t)
+        quant_pred(1, 0)
         resid(0, 0)
-        turn(2, 1)
-        resid(0, 1)
-        take(2, 0)
-        fit(0, 2)
-        quant_pred(1, 0, 4)
-        take(2, 1)
-        fit(0, 3)
-        turn(2, 2)
-        resid(0, 2)
-        turn(2, 3)
-        take(2, 2)
-        fit(1, 0)
-        resid(0, 3)
-        take(2, 3)
-        fit(1, 1)
-        resid(1, 0)
+        quant_pred(1, 1)
+        for t in range(1, 4):
+            resid(0, t)
+        for t in range(4):
+            fit(1, t, t)
+        for t in range(4):
+            take(2, t)
+        turn_var(7)
+        for t in range(3):
+            turn(3, t, 4 + t)
+        quant_pred(2, 0)
         inter_resid(0, 0)
-        turn(3, 0)
-        quant_pred(2, 0, 4)
-        fit(1, 2)
-        inter_resid(0, 1)
-        turn(3, 1)
-        turn(3, 2)
-        resid(1, 1)
-        take(3, 0)
-        fit(2, 0)
-        resid(1, 2)
-        take(3, 1)
-        fit(2, 1)
+        inter_resid(0, 1, True)
+        quant_pred(2, 1)
+        resid(1, 0)
+        take_var()
+        turn(3, 3, 7)
+        for t in range(1, 4):
+            resid(1, t)
+        for t in range(4):
+            fit(2, t, t)
         quant_resid(0, 0, 2)
-        take(3, 2)
-        turn(3, 3)
-        var_bank = psum.tile([P, P], BF16, name="tp", bufs=3)
-        nc.tensor.transpose(var_bank[:], var_rows[:], ident_b[:])
+        for t in range(4):
+            take(3, t)
+            score(4 + t, 0)
+        quant_pred(3, 0)
         resid(2, 0)
-        fit(1, 3)
-        take(3, 3)
-        resid(2, 1)
-        fit(2, 2)
-        resid(1, 3)
-        fit(2, 3)
-        quant_pred(3, 0, 4)
-        nc.vector.reciprocal(out=rvar[:], in_=var_bank[:, 0:NV])
-        nc.scalar.activation(out=rstd[:], in_=rvar[:], func=ACT.Sqrt)
+        quant_pred(3, 1)
         inter_resid(1, 0)
         inter_resid(1, 1)
-        resid(2, 2)
-        fit(3, 0)
-        resid(2, 3)
-        fit(3, 1)
-        resid(3, 0)
-        fit(3, 2)
-        inter_resid(2, 0)
+        for t in range(1, 4):
+            resid(2, t)
+        for t in range(4):
+            fit(3, t, t)
         quant_resid(1, 0, 2)
-        fit(3, 3)
+        inter_resid(2, 0)
         inter_resid(2, 1)
-        resid(3, 1)
-        resid(3, 2)
-        resid(3, 3)
+        for v in range(4, 8):
+            score(v, 1)
+        for t in range(4):
+            resid(3, t)
+            score(t, 0)
+            score(t, 1)
         quant_resid(2, 0, 2)
         inter_resid(3, 0)
         inter_resid(3, 1, True)
         quant_resid(3, 1, 2)
         quant_resid(3, 0, 1)
-        for v in range(8):
-            score(v, 0)
-            score(v, 1)
         for v in range(8):
             score(v, 2)
         for v in range(8):

@@ -46,6 +46,8 @@ def tile_gwas_score_statistics_s13_kernel(
 
         ident = kept([P, P], F32, "ident")
         make_identity(nc, ident[:])
+        ident_b = kept([P, P], BF16, "ident_b")
+        make_identity(nc, ident_b[:])
         var_rows = kept([P, P], BF16, "var_rows")
         nc.vector.memset(var_rows[0 : P - NV, :], 0.0)
         scale_parts = ((0, BANKS), (BANKS, NV))
@@ -123,7 +125,8 @@ def tile_gwas_score_statistics_s13_kernel(
             r_grp[g] = kept([P, TRAITS, PACK], BF16, "r_grp%d" % g)
             r_codes[g] = kept([P, TRAITS], U32, "r_codes%d" % g)
             r_sc[g] = kept([P, TRAITS], U8, "r_sc%d" % g)
-        sd_rows = kept([P, P], F32, "sd_rows")
+        var_cols = kept([P, NV], F32, "var_cols")
+        rvar = kept([P, NV], F32, "rvar")
         rstd = kept([P, NV], F32, "rstd")
 
         def copy(dst, src, on_vector):
@@ -132,15 +135,18 @@ def tile_gwas_score_statistics_s13_kernel(
             else:
                 nc.scalar.copy(out=dst, in_=src)
 
-        def root_var():
-            nc.scalar.activation(out=sd_rows[:], in_=var_rows[:], func=ACT.Sqrt)
-
         def turn_var(b):
-            turned["var"] = bank(b)
-            nc.tensor.transpose(turned["var"][:, 0:P], sd_rows[:], ident[:])
+            turned["var"] = psum.tile([P, P], BF16, name="bank%d" % b)
+            nc.tensor.transpose(turned["var"][:], var_rows[:], ident_b[:])
 
         def take_var():
-            nc.vector.reciprocal(out=rstd[:], in_=turned["var"][:, P - NV : P])
+            nc.scalar.copy(out=var_cols[:], in_=turned["var"][:, P - NV : P])
+
+        def invert_var():
+            nc.vector.reciprocal(out=rvar[:], in_=var_cols[:])
+
+        def root_var():
+            nc.scalar.activation(out=rstd[:], in_=rvar[:], func=ACT.Sqrt)
 
         def widen(h, t, on_vector=False):
             raw = e_bytes[h][:, t * TRAITS : (t + 1) * TRAITS].bitcast(FP8)
@@ -254,13 +260,14 @@ def tile_gwas_score_statistics_s13_kernel(
         load_pred(0, 1, 2)
         load_pred(0, 2, 4)
         load_pred(1, 0, 2)
-        load_pred(1, 2, 4)
         load_var()
-        load_traits(0)
+        load_pred(1, 2, 4)
         load_pred(2, 0, 2)
         load_pred(2, 2, 4)
         load_pred(3, 0, 2)
-        load_pred(3, 2, 4)
+        load_pred(3, 2, 3)
+        load_pred(3, 3, 4)
+        load_traits(0)
         load_traits(1)
         load_traits(2)
         load_scales(0)
@@ -273,8 +280,10 @@ def tile_gwas_score_statistics_s13_kernel(
 
         for t in range(4):
             turn(0, t, t)
-        for t in range(4):
-            turn(1, t, 4 + t)
+        turn(1, 0, 4)
+        turn(1, 1, 5)
+        turn_var(7)
+        turn(1, 2, 6)
         widen(0, 0)
         for t in range(1, 4):
             widen(0, t, True)
@@ -282,73 +291,71 @@ def tile_gwas_score_statistics_s13_kernel(
         take(0, 0)
         widen(1, 0)
         take(0, 1)
-        widen(1, 1)
-        widen(1, 2, True)
-        widen(1, 3, True)
+        for t in range(1, 4):
+            widen(1, t, True)
         quant_eff(0)
         take(0, 2)
         take(0, 3)
+        take(1, 0)
+        take_var()
+        turn(1, 3, 7)
         inter_eff(1, True)
         quant_pred(0, 0)
         quant_eff(1)
         quant_pred(0, 1)
+        invert_var()
         for t in range(4):
+            turn(2, t, t)
+        for t in range(1, 4):
             take(1, t)
         for t in range(4):
-            fit(0, t, t)
-        root_var()
-        for t in range(4):
-            turn(2, t, 4 + t)
+            turn(3, t, 4 + t)
         quant_pred(1, 0)
-        resid(0, 0)
         quant_pred(1, 1)
-        for t in range(1, 4):
-            resid(0, t)
-        for t in range(4):
-            fit(1, t, t)
         for t in range(4):
             take(2, t)
-        turn_var(7)
-        for t in range(3):
-            turn(3, t, 4 + t)
+            fit(0, t, t)
         quant_pred(2, 0)
-        inter_resid(0, 0)
-        inter_resid(0, 1, True)
         quant_pred(2, 1)
+        for t in range(4):
+            take(3, t)
+            fit(1, t, 4 + t)
+        root_var()
+        quant_pred(3, 0)
+        for t in range(4):
+            resid(0, t)
+            fit(2, t, t)
+        inter_resid(0, 0)
+        inter_resid(0, 1)
         resid(1, 0)
-        take_var()
-        turn(3, 3, 7)
+        quant_pred(3, 1)
         for t in range(1, 4):
             resid(1, t)
         for t in range(4):
-            fit(2, t, t)
-        quant_resid(0, 0, 2)
-        for t in range(4):
-            take(3, t)
-            score(4 + t, 0)
-        quant_pred(3, 0)
-        resid(2, 0)
-        quant_pred(3, 1)
+            fit(3, t, 4 + t)
         inter_resid(1, 0)
         inter_resid(1, 1)
+        resid(2, 0)
+        quant_resid(0, 0, 2)
         for t in range(1, 4):
             resid(2, t)
-        for t in range(4):
-            fit(3, t, t)
-        quant_resid(1, 0, 2)
         inter_resid(2, 0)
         inter_resid(2, 1)
-        for v in range(4, 8):
-            score(v, 1)
+        for v in range(4):
+            score(v, 0)
+        quant_resid(1, 0, 2)
         for t in range(4):
             resid(3, t)
-            score(t, 0)
-            score(t, 1)
-        quant_resid(2, 0, 2)
+        for v in range(4):
+            score(v, 1)
+        for v in range(4, 8):
+            score(v, 0)
+            score(v, 1)
         inter_resid(3, 0)
+        quant_resid(2, 0, 2)
         inter_resid(3, 1, True)
-        quant_resid(3, 1, 2)
         quant_resid(3, 0, 1)
+        quant_resid(3, 1, 2)
         for v in range(8):
             score(v, 2)
         for v in range(8):

@@ -50,7 +50,7 @@ def tile_gwas_score_statistics_s13_kernel(
         make_identity(nc, ident_b[:])
         var_rows = kept([P, P], BF16, "var_rows")
         nc.vector.memset(var_rows[0 : P - NV, :], 0.0)
-        scale_parts = ((0, BANKS), (BANKS, NV))
+        scale_parts = tuple((v0, v0 + BANKS) for v0 in range(0, NV, BANKS))
         g_scales = []
         for v0, v1 in scale_parts:
             gs = kept([P, G, (v1 - v0) * P], U8, "g_scales%d" % v0)
@@ -228,7 +228,7 @@ def tile_gwas_score_statistics_s13_kernel(
         def score(v, g):
             if g == 0:
                 scored[v] = bank(v % BANKS)
-            part = 0 if v < BANKS else 1
+            part = v // BANKS
             col = (v - scale_parts[part][0]) * P
             nc.tensor.matmul_mx(
                 out=scored[v][:],
@@ -274,9 +274,10 @@ def tile_gwas_score_statistics_s13_kernel(
         load_words(0, 8, 0, 2)
         load_traits(3)
         load_words(0, 8, 2, 4)
-        load_scales(1)
-        load_words(8, 16, 0, 4)
-        load_words(16, 24, 0, 4)
+        for part in range(1, 3):
+            load_scales(part)
+            load_words(8 * part, 8 * part + 4, 0, 4)
+            load_words(8 * part + 4, 8 * part + 8, 0, 4)
 
         for t in range(4):
             turn(0, t, t)

@@ -225,42 +225,51 @@ def tile_gwas_score_statistics_s13_kernel(
                 in_=r_grp[g][:, cols, :].rearrange("p n t -> p (n t)"),
             )
 
-        def score(v, g):
-            if g == 0:
-                scored[v] = bank(v % BANKS)
+        def score_pass(v, g, acc, cols):
             part = v // BANKS
             col = (v - scale_parts[part][0]) * P
             nc.tensor.matmul_mx(
-                out=scored[v][:],
+                out=acc,
                 lhsT=g_words[v, g].bitcast(FP4X4),
                 lhsT_scale=g_scales[part][:, g, col : col + P],
-                rhs=r_codes[g][:].bitcast(FP8X4),
-                rhs_scale=r_sc[g][:],
+                rhs=r_codes[g][:, cols].bitcast(FP8X4),
+                rhs_scale=r_sc[g][:, cols],
                 start=(g == 0),
                 stop=(g == G - 1),
             )
 
+        def score(v, g):
+            if g == 0:
+                scored[v] = bank(v % BANKS)
+            score_pass(v, g, scored[v][:], slice(0, TRAITS))
+
+        def store(v, acc, res, cols):
+            nc.scalar.activation(out=res, in_=acc, func=ACT.Square, scale=rstd[:, v : v + 1])
+            nc.sync.dma_start(out=out[v * P : (v + 1) * P, cols], in_=res)
+
         def finish(v):
             res = work.tile([P, TRAITS], F32, name="res")
-            parts = 2 if v == NV - 1 else 1
-            width = TRAITS // parts
+            parts = 2 if v == NV - 2 else 1
             for i in range(parts):
-                cols = slice(i * width, (i + 1) * width)
-                nc.scalar.activation(
-                    out=res[:, cols],
-                    in_=scored[v][:, cols],
-                    func=ACT.Square,
-                    scale=rstd[:, v : v + 1],
-                )
-                nc.sync.dma_start(out=out[v * P : (v + 1) * P, cols], in_=res[:, cols])
+                cols = slice(i * TRAITS // parts, (i + 1) * TRAITS // parts)
+                store(v, scored[v][:, cols], res[:, cols], cols)
+
+        def last_tile(v):
+            for q in range(4):
+                cols = slice(q * P, (q + 1) * P)
+                acc = psum.tile([P, P], F32, name="bank%d" % ((v + q) % BANKS))
+                for g in range(G):
+                    score_pass(v, g, acc[:], cols)
+                res = kept([P, P], F32, "last%d" % q)
+                store(v, acc[:], res[:], cols)
 
         load_eff(0)
         load_pred(0, 0, 1)
         load_eff(1)
+        load_var()
         load_pred(0, 1, 2)
         load_pred(0, 2, 4)
         load_pred(1, 0, 2)
-        load_var()
         load_pred(1, 2, 4)
         load_pred(2, 0, 2)
         load_pred(2, 2, 4)
@@ -279,12 +288,13 @@ def tile_gwas_score_statistics_s13_kernel(
             load_words(8 * part, 8 * part + 4, 0, 4)
             load_words(8 * part + 4, 8 * part + 8, 0, 4)
 
-        for t in range(4):
-            turn(0, t, t)
-        turn(1, 0, 4)
-        turn(1, 1, 5)
+        turn(0, 0, 0)
+        turn(0, 1, 1)
         turn_var(7)
-        turn(1, 2, 6)
+        turn(0, 2, 2)
+        turn(0, 3, 3)
+        for t in range(3):
+            turn(1, t, 4 + t)
         widen(0, 0)
         for t in range(1, 4):
             widen(0, t, True)
@@ -292,13 +302,13 @@ def tile_gwas_score_statistics_s13_kernel(
         take(0, 0)
         widen(1, 0)
         take(0, 1)
+        take_var()
         for t in range(1, 4):
             widen(1, t, True)
         quant_eff(0)
         take(0, 2)
         take(0, 3)
         take(1, 0)
-        take_var()
         turn(1, 3, 7)
         inter_eff(1, True)
         quant_pred(0, 0)
@@ -323,14 +333,13 @@ def tile_gwas_score_statistics_s13_kernel(
             fit(1, t, 4 + t)
         root_var()
         quant_pred(3, 0)
+        quant_pred(3, 1)
         for t in range(4):
             resid(0, t)
             fit(2, t, t)
         inter_resid(0, 0)
         inter_resid(0, 1)
-        resid(1, 0)
-        quant_pred(3, 1)
-        for t in range(1, 4):
+        for t in range(4):
             resid(1, t)
         for t in range(4):
             fit(3, t, 4 + t)
@@ -362,7 +371,8 @@ def tile_gwas_score_statistics_s13_kernel(
         for v in range(8):
             score(v, 3)
             finish(v)
-        for v in range(8, NV):
+        for v in range(8, NV - 1):
             for g in range(G):
                 score(v, g)
             finish(v)
+        last_tile(NV - 1)

@@ -125,7 +125,6 @@ def tile_gwas_score_statistics_s13_kernel(
             r_grp[g] = kept([P, TRAITS, PACK], BF16, "r_grp%d" % g)
             r_codes[g] = kept([P, TRAITS], U32, "r_codes%d" % g)
             r_sc[g] = kept([P, TRAITS], U8, "r_sc%d" % g)
-        var_cols = kept([P, NV], F32, "var_cols")
         rvar = kept([P, NV], F32, "rvar")
         rstd = kept([P, NV], F32, "rstd")
 
@@ -136,14 +135,11 @@ def tile_gwas_score_statistics_s13_kernel(
                 nc.scalar.copy(out=dst, in_=src)
 
         def turn_var(b):
-            turned["var"] = psum.tile([P, P], BF16, name="bank%d" % b)
-            nc.tensor.transpose(turned["var"][:], var_rows[:], ident_b[:])
-
-        def take_var():
-            nc.scalar.copy(out=var_cols[:], in_=turned["var"][:, P - NV : P])
+            turned["var"] = psum.tile([P, P], F32, name="bank%d" % b)
+            nc.tensor.matmul(turned["var"][:], lhsT=var_rows[:], rhs=ident_b[:], start=True, stop=True)
 
         def invert_var():
-            nc.vector.reciprocal(out=rvar[:], in_=var_cols[:])
+            nc.vector.reciprocal(out=rvar[:], in_=turned["var"][:, P - NV : P])
 
         def root_var():
             nc.scalar.activation(out=rstd[:], in_=rvar[:], func=ACT.Sqrt)
@@ -266,11 +262,11 @@ def tile_gwas_score_statistics_s13_kernel(
         load_eff(0)
         load_pred(0, 0, 1)
         load_eff(1)
-        load_var()
         load_pred(0, 1, 2)
         load_pred(0, 2, 4)
         load_pred(1, 0, 2)
         load_pred(1, 2, 4)
+        load_var()
         load_pred(2, 0, 2)
         load_pred(2, 2, 4)
         load_pred(3, 0, 2)
@@ -290,7 +286,6 @@ def tile_gwas_score_statistics_s13_kernel(
 
         turn(0, 0, 0)
         turn(0, 1, 1)
-        turn_var(7)
         turn(0, 2, 2)
         turn(0, 3, 3)
         for t in range(3):
@@ -302,7 +297,6 @@ def tile_gwas_score_statistics_s13_kernel(
         take(0, 0)
         widen(1, 0)
         take(0, 1)
-        take_var()
         for t in range(1, 4):
             widen(1, t, True)
         quant_eff(0)
@@ -314,7 +308,6 @@ def tile_gwas_score_statistics_s13_kernel(
         quant_pred(0, 0)
         quant_eff(1)
         quant_pred(0, 1)
-        invert_var()
         for t in range(4):
             turn(2, t, t)
         for t in range(1, 4):
@@ -325,15 +318,19 @@ def tile_gwas_score_statistics_s13_kernel(
         quant_pred(1, 1)
         for t in range(4):
             take(2, t)
-            fit(0, t, t)
+        turn_var(3)
         quant_pred(2, 0)
         quant_pred(2, 1)
         for t in range(4):
             take(3, t)
-            fit(1, t, 4 + t)
-        root_var()
         quant_pred(3, 0)
+        invert_var()
         quant_pred(3, 1)
+        root_var()
+        for t in range(4):
+            fit(0, t, t)
+        for t in range(4):
+            fit(1, t, 4 + t)
         for t in range(4):
             resid(0, t)
             fit(2, t, t)

@@ -99,13 +99,13 @@ def tile_gwas_score_statistics_s13_kernel(
 
         scale_rows = geno_scales.bitcast(I32).rearrange("g (q r) n -> r q g n", r=4)
 
-        def load_scales(part):
+        def load_scales(part, g0=0, g1=G):
             v0, v1 = scale_parts[part]
             dst = g_scales[part][:].rearrange("p g n -> p (g n)").bitcast(I32)
             dst = dst.rearrange("p (g n) -> p g n", g=G)
             for r in range(4):
                 nc.sync.dma_start(
-                    out=dst[r:P:QUAD, :, :], in_=scale_rows[r][:, :, v0 * P // 4 : v1 * P // 4]
+                    out=dst[r:P:QUAD, g0:g1, :], in_=scale_rows[r][:, g0:g1, v0 * P // 4 : v1 * P // 4]
                 )
 
         e_wide, e_grp, e_codes, e_sc = {}, {}, {}, {}
@@ -260,9 +260,8 @@ def tile_gwas_score_statistics_s13_kernel(
                 store(v, acc[:], res[:], cols)
 
         load_eff(0)
-        load_pred(0, 0, 1)
+        load_pred(0, 0, 2)
         load_eff(1)
-        load_pred(0, 1, 2)
         load_pred(0, 2, 4)
         load_pred(1, 0, 2)
         load_pred(1, 2, 4)
@@ -275,9 +274,10 @@ def tile_gwas_score_statistics_s13_kernel(
         load_traits(0)
         load_traits(1)
         load_traits(2)
-        load_scales(0)
+        load_scales(0, 0, 2)
         load_words(0, 8, 0, 2)
         load_traits(3)
+        load_scales(0, 2, 4)
         load_words(0, 8, 2, 4)
         for part in range(1, 3):
             load_scales(part)

@@ -245,7 +245,7 @@ def tile_gwas_score_statistics_s13_kernel(
 
         def finish(v):
             res = work.tile([P, TRAITS], F32, name="res")
-            parts = 2 if v == NV - 2 else 1
+            parts = 2 if v >= NV - 6 else 1
             for i in range(parts):
                 cols = slice(i * TRAITS // parts, (i + 1) * TRAITS // parts)
                 store(v, scored[v][:, cols], res[:, cols], cols)

@@ -39,7 +39,7 @@ def tile_gwas_score_statistics_s13_kernel(
         ctx.enter_context(tc.manual_schedule())
 
         def kept(shape, dtype, name):
-            return keep.tile(shape, dtype, name=name, align_bytes=64)
+            return keep.tile(shape, dtype, name=name, align_bytes=256)
 
         def bank(b):
             return psum.tile([P, TRAITS], F32, name="bank%d" % b)

@@ -26,6 +26,9 @@ NV = VARIANTS // P
 HALF = TRAITS // 2
 BANKS = 8
 QUAD = 32
+RESULT_BUFS = 8
+STAGE_BUFS = 4
+HALVED_FROM = NV - 6
 
 
 def tile_gwas_score_statistics_s13_kernel(
@@ -34,7 +37,8 @@ def tile_gwas_score_statistics_s13_kernel(
     nc = tc.nc
     with ExitStack() as ctx:
         keep = ctx.enter_context(tc.tile_pool(name="keep", bufs=1))
-        work = ctx.enter_context(tc.tile_pool(name="work", bufs=6))
+        work = ctx.enter_context(tc.tile_pool(name="work", bufs=RESULT_BUFS))
+        stage = ctx.enter_context(tc.tile_pool(name="stage", bufs=STAGE_BUFS))
         psum = ctx.enter_context(tc.psum_pool(name="psum", bufs=1))
         ctx.enter_context(tc.manual_schedule())
 
@@ -66,7 +70,7 @@ def tile_gwas_score_statistics_s13_kernel(
         def load_var():
             nc.sync.dma_start(out=var_rows[P - NV : P, :], in_=var.rearrange("(j p) -> j p", p=P))
 
-        e_bytes, p_raw, t_raw, g_words = {}, {}, {}, {}
+        e_bytes, p_raw, p_pair, t_raw, g_words = {}, {}, {}, {}, {}
 
         def load_eff(h):
             e_bytes[h] = kept([P, PACK * TRAITS], U8, "e_bytes%d" % h)
@@ -81,6 +85,7 @@ def tile_gwas_score_statistics_s13_kernel(
         def load_pred(g, t0, t1):
             raw = kept([P, t1 - t0, PRED], BF16, "p_raw%d_%d" % (g, t0))
             nc.sync.dma_start(out=raw[:], in_=pred_v[g, :, t0:t1, :])
+            p_pair[g, t0 // 2] = raw
             for t in range(t0, t1):
                 p_raw[g, t] = raw[:, t - t0, :]
 
@@ -110,19 +115,19 @@ def tile_gwas_score_statistics_s13_kernel(
 
         e_wide, e_grp, e_codes, e_sc = {}, {}, {}, {}
         for h in range(H):
-            e_wide[h] = kept([P, PACK, TRAITS], BF16, "e_wide%d" % h)
-            e_grp[h] = kept([P, TRAITS, PACK], BF16, "e_grp%d" % h)
-            e_codes[h] = kept([P, TRAITS], U32, "e_codes%d" % h)
-            e_sc[h] = kept([P, TRAITS], U8, "e_sc%d" % h)
-        p_grp, p_codes, p_sc = {}, {}, {}
-        r_plain, r_grp, r_codes, r_sc = {}, {}, {}, {}
+            for c in range(2):
+                e_wide[h, c] = kept([P, PACK, HALF], BF16, "e_wide%d_%d" % (h, c))
+                e_grp[h, c] = kept([P, HALF, PACK], BF16, "e_grp%d_%d" % (h, c))
+                e_codes[h, c] = kept([P, HALF], U32, "e_codes%d_%d" % (h, c))
+                e_sc[h, c] = kept([P, HALF], U8, "e_sc%d_%d" % (h, c))
+        p_sorted, p_grp, p_codes, p_sc = {}, {}, {}, {}
+        r_pairs, r_grp, r_codes, r_sc = {}, {}, {}, {}
         for g in range(G):
             for a in range(2):
-                p_grp[g, a] = kept([P, 2, H, P, PACK], BF16, "p_grp%d_%d" % (g, a))
                 p_codes[g, a] = kept([P, 2, H, P], U32, "p_codes%d_%d" % (g, a))
                 p_sc[g, a] = kept([P, 2, H, P], U8, "p_sc%d_%d" % (g, a))
-            r_plain[g] = kept([P, PACK, TRAITS], BF16, "r_plain%d" % g)
-            r_grp[g] = kept([P, TRAITS, PACK], BF16, "r_grp%d" % g)
+            for c in range(2):
+                r_grp[g, c] = kept([P, HALF, PACK], BF16, "r_grp%d_%d" % (g, c))
             r_codes[g] = kept([P, TRAITS], U32, "r_codes%d" % g)
             r_sc[g] = kept([P, TRAITS], U8, "r_sc%d" % g)
         rvar = kept([P, NV], F32, "rvar")
@@ -134,6 +139,8 @@ def tile_gwas_score_statistics_s13_kernel(
             else:
                 nc.scalar.copy(out=dst, in_=src)
 
+        turned, fitted, spilled, scored = {}, {}, {}, {}
+
         def turn_var(b):
             turned["var"] = psum.tile([P, P], F32, name="bank%d" % b)
             nc.tensor.matmul(turned["var"][:], lhsT=var_rows[:], rhs=ident_b[:], start=True, stop=True)
@@ -144,32 +151,28 @@ def tile_gwas_score_statistics_s13_kernel(
         def root_var():
             nc.scalar.activation(out=rstd[:], in_=rvar[:], func=ACT.Sqrt)
 
-        def widen(h, t, on_vector=False):
-            raw = e_bytes[h][:, t * TRAITS : (t + 1) * TRAITS].bitcast(FP8)
+        def widen(h, t, on_vector, c):
+            col = t * TRAITS + c * HALF
+            raw = e_bytes[h][:, col : col + HALF].bitcast(FP8)
             scale = e_scale[:, h * PACK + t : h * PACK + t + 1]
             if on_vector:
                 nc.vector.tensor_scalar(
-                    out=e_wide[h][:, t, :], in0=raw, scalar1=scale, scalar2=None, op0=ALU.mult
+                    out=e_wide[h, c][:, t, :], in0=raw, scalar1=scale, scalar2=None, op0=ALU.mult
                 )
             else:
-                nc.scalar.activation(out=e_wide[h][:, t, :], in_=raw, func=ACT.Copy, scale=scale)
+                nc.scalar.activation(out=e_wide[h, c][:, t, :], in_=raw, func=ACT.Copy, scale=scale)
 
-        def interleave(dst, src, on_vector):
-            dst = dst.rearrange("p (c i) t -> p c t i", i=4)
-            src = src.rearrange("p t (c i) -> p c t i", i=4)
+        def inter_eff(h, on_vector, c):
+            dst = e_grp[h, c][:].rearrange("p (n i) t -> p n t i", i=4)
+            src = e_wide[h, c][:].rearrange("p t (n i) -> p n t i", i=4)
             copy(dst, src, on_vector)
 
-        def inter_eff(h, on_vector=False):
-            interleave(e_grp[h][:], e_wide[h][:], on_vector)
-
-        def quant_eff(h):
+        def quant_eff(h, c):
             nc.vector.quantize_mx(
-                out=e_codes[h][:].bitcast(FP8X4),
-                scales=e_sc[h][:],
-                in_=e_grp[h][:].rearrange("p n t -> p (n t)"),
+                out=e_codes[h, c][:].bitcast(FP8X4),
+                scales=e_sc[h, c][:],
+                in_=e_grp[h, c][:].rearrange("p n t -> p (n t)"),
             )
-
-        turned, fitted, scored = {}, {}, {}
 
         def turn(g, t, b):
             turned[g, t] = bank(b)[:].rearrange("p (h u r) -> p h u r", h=H, u=2)
@@ -179,7 +182,21 @@ def tile_gwas_score_statistics_s13_kernel(
                     src = words[:, 256 * h + u : 256 * (h + 1) : 2]
                     nc.tensor.transpose(turned[g, t][:, h, u, :], src, ident[:])
 
+        def sort(g, a, on_vector=False):
+            p_sorted[g, a] = kept([P, 2 * H, 2, P], F32, "p_sorted%d_%d" % (g, a))
+            words = p_pair[g, a][:].rearrange("p t k -> p (t k)").bitcast(F32)
+            copy(p_sorted[g, a][:], words.rearrange("p (s w u) -> p s u w", u=2, w=P), on_vector)
+
+        def turn_sorted(g, t, b):
+            turned[g, t] = bank(b)[:].rearrange("p (h u r) -> p h u r", h=H, u=2)
+            for h in range(H):
+                for u in range(2):
+                    src = p_sorted[g, t // 2][:, (t % 2) * H + h, u, :]
+                    nc.tensor.transpose(turned[g, t][:, h, u, :], src, ident[:])
+
         def take(g, t, on_vector=False):
+            if t % 2 == 0:
+                p_grp[g, t // 2] = stage.tile([P, 2, H, P, PACK], BF16, name="p_grp", align_bytes=256)
             dst = p_grp[g, t // 2][:, t % 2, :, :, :].rearrange("p h r j -> p (h r j)").bitcast(F32)
             dst = dst.rearrange("p (h r u) -> p h r u", h=H, u=2)
             copy(dst, turned[g, t].rearrange("p h u r -> p h r u"), on_vector)
@@ -191,34 +208,50 @@ def tile_gwas_score_statistics_s13_kernel(
                 in_=p_grp[g, a][:].rearrange("p t h r j -> p (t h r j)"),
             )
 
-        def fit(g, t, b):
-            fitted[g, t] = bank(b)
-            for h in range(H):
+        def fit_pair(g, a, c, h, b):
+            if h == 0:
+                fitted[g, a, c] = bank(b)
+            for e in range(2):
                 nc.tensor.matmul_mx(
-                    out=fitted[g, t][:],
-                    lhsT=p_codes[g, t // 2][:, t % 2, h, :].bitcast(FP8X4),
-                    lhsT_scale=p_sc[g, t // 2][:, t % 2, h, :],
-                    rhs=e_codes[h][:].bitcast(FP8X4),
-                    rhs_scale=e_sc[h][:],
-                    start=(h == 0),
-                    stop=(h == H - 1),
+                    out=fitted[g, a, c][:, e * HALF : (e + 1) * HALF],
+                    lhsT=p_codes[g, a][:, e, h, :].bitcast(FP8X4),
+                    lhsT_scale=p_sc[g, a][:, e, h, :],
+                    rhs=e_codes[h, c][:].bitcast(FP8X4),
+                    rhs_scale=e_sc[h, c][:],
+                    start=(h == 0 and e == 0),
+                    stop=(h == H - 1 and e == 1),
                 )
 
-        def resid(g, t):
+        def spill_pair(g, a, c):
+            spilled[g, a, c] = stage.tile([P, HALF, 2], F32, name="spilled", align_bytes=256)
+            nc.scalar.copy(out=spilled[g, a, c][:], in_=fitted[g, a, c][:].rearrange("p (e n) -> p n e", e=2))
+
+        def resid_pair(g, a, c):
+            if (g, c) not in r_pairs:
+                r_pairs[g, c] = stage.tile([P, 2, HALF, 2], BF16, name="r_pairs", align_bytes=256)
+            if (g, a, c) in spilled:
+                fit_pairs = spilled[g, a, c][:]
+            else:
+                fit_pairs = fitted[g, a, c][:].rearrange("p (e n) -> p n e", e=2)
+            rows = t_raw[g][:, 2 * a : 2 * a + 2, c * HALF : (c + 1) * HALF]
             nc.vector.tensor_tensor(
-                out=r_plain[g][:, t, :], in0=t_raw[g][:, t, :], in1=fitted[g, t][:], op=ALU.subtract
+                out=r_pairs[g, c][:, a, :, :],
+                in0=rows.rearrange("p e n -> p n e"),
+                in1=fit_pairs,
+                op=ALU.subtract,
             )
 
-        def inter_resid(g, a, on_vector=False):
-            cols = slice(a * HALF, (a + 1) * HALF)
-            interleave(r_grp[g][:, cols, :], r_plain[g][:, :, cols], on_vector)
+        def weave(g, c, on_vector=False):
+            dst = r_grp[g, c][:].rearrange("p n t -> p (n t)").bitcast(F32)
+            src = r_pairs[g, c][:].rearrange("p a n e -> p (a n e)").bitcast(F32)
+            copy(dst.rearrange("p (n a) -> p n a", a=2), src.rearrange("p (a n) -> p n a", a=2), on_vector)
 
-        def quant_resid(g, a0, a1):
-            cols = slice(a0 * HALF, a1 * HALF)
+        def quant_resid(g, c):
+            cols = slice(c * HALF, (c + 1) * HALF)
             nc.vector.quantize_mx(
                 out=r_codes[g][:, cols].bitcast(FP8X4),
                 scales=r_sc[g][:, cols],
-                in_=r_grp[g][:, cols, :].rearrange("p n t -> p (n t)"),
+                in_=r_grp[g, c][:].rearrange("p n t -> p (n t)"),
             )
 
         def score_pass(v, g, acc, cols):
@@ -245,7 +278,7 @@ def tile_gwas_score_statistics_s13_kernel(
 
         def finish(v):
             res = work.tile([P, TRAITS], F32, name="res")
-            parts = 2 if v >= NV - 6 else 1
+            parts = 2 if v >= HALVED_FROM else 1
             for i in range(parts):
                 cols = slice(i * TRAITS // parts, (i + 1) * TRAITS // parts)
                 store(v, scored[v][:, cols], res[:, cols], cols)
@@ -261,17 +294,17 @@ def tile_gwas_score_statistics_s13_kernel(
 
         load_eff(0)
         load_pred(0, 0, 2)
-        load_eff(1)
         load_pred(0, 2, 4)
         load_pred(1, 0, 2)
         load_pred(1, 2, 4)
         load_var()
         load_pred(2, 0, 2)
-        load_pred(2, 2, 4)
-        load_pred(3, 0, 2)
-        load_pred(3, 2, 3)
-        load_pred(3, 3, 4)
+        load_pred(2, 2, 3)
+        load_pred(2, 3, 4)
+        load_eff(1)
         load_traits(0)
+        load_pred(3, 0, 2)
+        load_pred(3, 2, 4)
         load_traits(1)
         load_traits(2)
         load_scales(0, 0, 2)
@@ -283,86 +316,99 @@ def tile_gwas_score_statistics_s13_kernel(
             load_scales(part)
             load_words(8 * part, 8 * part + 4, 0, 4)
             load_words(8 * part + 4, 8 * part + 8, 0, 4)
-
-        turn(0, 0, 0)
-        turn(0, 1, 1)
-        turn(0, 2, 2)
-        turn(0, 3, 3)
-        for t in range(3):
+        pairs = [(a, c) for c in range(2) for a in range(2)]
+        for t in range(4):
+            turn(0, t, t)
+        for t in range(4):
             turn(1, t, 4 + t)
-        widen(0, 0)
-        for t in range(1, 4):
-            widen(0, t, True)
-        inter_eff(0, True)
-        take(0, 0)
-        widen(1, 0)
-        take(0, 1)
-        for t in range(1, 4):
-            widen(1, t, True)
-        quant_eff(0)
-        take(0, 2)
-        take(0, 3)
-        take(1, 0)
-        turn(1, 3, 7)
-        inter_eff(1, True)
+        for c in range(2):
+            for t in range(4):
+                widen(0, t, True, c)
+        for c in range(2):
+            inter_eff(0, True, c)
+        for c in range(2):
+            quant_eff(0, c)
+        for t in range(4):
+            take(0, t)
         quant_pred(0, 0)
-        quant_eff(1)
         quant_pred(0, 1)
         for t in range(4):
             turn(2, t, t)
-        for t in range(1, 4):
-            take(1, t)
         for t in range(4):
-            turn(3, t, 4 + t)
+            take(1, t)
+        turn_var(7)
         quant_pred(1, 0)
         quant_pred(1, 1)
         for t in range(4):
             take(2, t)
-        turn_var(3)
+        for c in range(2):
+            for t in range(4):
+                widen(1, t, True, c)
+        inter_eff(1, True, 0)
+        inter_eff(1, False, 1)
+        invert_var()
+        root_var()
+        quant_eff(1, 0)
         quant_pred(2, 0)
+        quant_eff(1, 1)
         quant_pred(2, 1)
+        sort(3, 0)
+        sort(3, 1)
+        for h in range(2):
+            for g in range(2):
+                for i, (a, c) in enumerate(pairs):
+                    fit_pair(g, a, c, h, (4 + 4 * g + i) % 8)
+        for a, c in pairs:
+            resid_pair(0, a, c)
+        for t in range(4):
+            turn_sorted(3, t, 4 + t)
+        for a, c in pairs:
+            resid_pair(1, a, c)
         for t in range(4):
             take(3, t)
+        for i, (a, c) in enumerate(pairs):
+            for h in range(2):
+                fit_pair(2, a, c, h, i)
+        weave(0, 0)
+        weave(0, 1)
+        weave(1, 0)
+        weave(1, 1)
         quant_pred(3, 0)
-        invert_var()
         quant_pred(3, 1)
-        root_var()
-        for t in range(4):
-            fit(0, t, t)
-        for t in range(4):
-            fit(1, t, 4 + t)
-        for t in range(4):
-            resid(0, t)
-            fit(2, t, t)
-        inter_resid(0, 0)
-        inter_resid(0, 1)
-        for t in range(4):
-            resid(1, t)
-        for t in range(4):
-            fit(3, t, 4 + t)
-        inter_resid(1, 0)
-        inter_resid(1, 1)
-        resid(2, 0)
-        quant_resid(0, 0, 2)
-        for t in range(1, 4):
-            resid(2, t)
-        inter_resid(2, 0)
-        inter_resid(2, 1)
-        for v in range(4):
-            score(v, 0)
-        quant_resid(1, 0, 2)
-        for t in range(4):
-            resid(3, t)
-        for v in range(4):
-            score(v, 1)
+        for i, (a, c) in enumerate([(0, 0), (0, 1), (1, 0), (1, 1)]):
+            for h in range(2):
+                fit_pair(3, a, c, h, 4 + i)
+        quant_resid(0, 0)
+        quant_resid(0, 1)
+        resid_pair(2, 0, 0)
+        spill_pair(2, 0, 1)
+        spill_pair(2, 1, 1)
+        quant_resid(1, 0)
+        quant_resid(1, 1)
+        resid_pair(2, 1, 0)
+        resid_pair(2, 0, 1)
+        resid_pair(2, 1, 1)
+        spill_pair(3, 0, 0)
+        weave(2, 0)
+        spill_pair(3, 0, 1)
+        weave(2, 1)
+        resid_pair(3, 1, 0)
+        quant_resid(2, 0)
+        resid_pair(3, 1, 1)
+        quant_resid(2, 1)
+        resid_pair(3, 0, 0)
+        resid_pair(3, 0, 1)
+        weave(3, 0)
+        weave(3, 1)
+        quant_resid(3, 0)
+        quant_resid(3, 1)
+        for first, second in ((0, 2), (1, 3)):
+            for g in range(2):
+                score(first, g)
+                score(second, g)
         for v in range(4, 8):
             score(v, 0)
             score(v, 1)
-        inter_resid(3, 0)
-        quant_resid(2, 0, 2)
-        inter_resid(3, 1, True)
-        quant_resid(3, 0, 1)
-        quant_resid(3, 1, 2)
         for v in range(8):
             score(v, 2)
         for v in range(8):

@@ -70,7 +70,7 @@ def tile_gwas_score_statistics_s13_kernel(
         def load_var():
             nc.sync.dma_start(out=var_rows[P - NV : P, :], in_=var.rearrange("(j p) -> j p", p=P))
 
-        e_bytes, p_raw, p_pair, t_raw, g_words = {}, {}, {}, {}, {}
+        e_bytes, p_raw, t_raw, g_words = {}, {}, {}, {}
 
         def load_eff(h):
             e_bytes[h] = kept([P, PACK * TRAITS], U8, "e_bytes%d" % h)
@@ -85,7 +85,6 @@ def tile_gwas_score_statistics_s13_kernel(
         def load_pred(g, t0, t1):
             raw = kept([P, t1 - t0, PRED], BF16, "p_raw%d_%d" % (g, t0))
             nc.sync.dma_start(out=raw[:], in_=pred_v[g, :, t0:t1, :])
-            p_pair[g, t0 // 2] = raw
             for t in range(t0, t1):
                 p_raw[g, t] = raw[:, t - t0, :]
 
@@ -162,9 +161,9 @@ def tile_gwas_score_statistics_s13_kernel(
             else:
                 nc.scalar.activation(out=e_wide[h, c][:, t, :], in_=raw, func=ACT.Copy, scale=scale)
 
-        def inter_eff(h, on_vector, c):
-            dst = e_grp[h, c][:].rearrange("p (n i) t -> p n t i", i=4)
-            src = e_wide[h, c][:].rearrange("p t (n i) -> p n t i", i=4)
+        def inter_eff(h, on_vector, c, lo=0, hi=HALF):
+            dst = e_grp[h, c][:, lo:hi, :].rearrange("p (n i) t -> p n t i", i=4)
+            src = e_wide[h, c][:, :, lo:hi].rearrange("p t (n i) -> p n t i", i=4)
             copy(dst, src, on_vector)
 
         def quant_eff(h, c):
@@ -182,16 +181,16 @@ def tile_gwas_score_statistics_s13_kernel(
                     src = words[:, 256 * h + u : 256 * (h + 1) : 2]
                     nc.tensor.transpose(turned[g, t][:, h, u, :], src, ident[:])
 
-        def sort(g, a, on_vector=False):
-            p_sorted[g, a] = kept([P, 2 * H, 2, P], F32, "p_sorted%d_%d" % (g, a))
-            words = p_pair[g, a][:].rearrange("p t k -> p (t k)").bitcast(F32)
-            copy(p_sorted[g, a][:], words.rearrange("p (s w u) -> p s u w", u=2, w=P), on_vector)
+        def sort_slot(g, t, on_vector=False):
+            p_sorted[g, t] = kept([P, H, 2, P], F32, "p_sorted%d_%d" % (g, t))
+            words = p_raw[g, t].bitcast(F32)
+            copy(p_sorted[g, t][:], words.rearrange("p (h w u) -> p h u w", u=2, w=P), on_vector)
 
         def turn_sorted(g, t, b):
             turned[g, t] = bank(b)[:].rearrange("p (h u r) -> p h u r", h=H, u=2)
             for h in range(H):
                 for u in range(2):
-                    src = p_sorted[g, t // 2][:, (t % 2) * H + h, u, :]
+                    src = p_sorted[g, t][:, h, u, :]
                     nc.tensor.transpose(turned[g, t][:, h, u, :], src, ident[:])
 
         def take(g, t, on_vector=False):
@@ -303,9 +302,10 @@ def tile_gwas_score_statistics_s13_kernel(
         load_pred(2, 3, 4)
         load_eff(1)
         load_traits(0)
-        load_pred(3, 0, 2)
-        load_pred(3, 2, 4)
         load_traits(1)
+        load_pred(3, 0, 2)
+        load_pred(3, 2, 3)
+        load_pred(3, 3, 4)
         load_traits(2)
         load_scales(0, 0, 2)
         load_words(0, 8, 0, 2)
@@ -316,7 +316,6 @@ def tile_gwas_score_statistics_s13_kernel(
             load_scales(part)
             load_words(8 * part, 8 * part + 4, 0, 4)
             load_words(8 * part + 4, 8 * part + 8, 0, 4)
-        pairs = [(a, c) for c in range(2) for a in range(2)]
         for t in range(4):
             turn(0, t, t)
         for t in range(4):
@@ -332,85 +331,104 @@ def tile_gwas_score_statistics_s13_kernel(
             take(0, t)
         quant_pred(0, 0)
         quant_pred(0, 1)
+        turn_var(3)
+        take(1, 0)
+        take(1, 1)
+        quant_pred(1, 0)
+        invert_var()
         for t in range(4):
             turn(2, t, t)
-        for t in range(4):
-            take(1, t)
-        turn_var(7)
-        quant_pred(1, 0)
+        take(1, 2)
+        take(1, 3)
         quant_pred(1, 1)
         for t in range(4):
             take(2, t)
-        for c in range(2):
-            for t in range(4):
-                widen(1, t, True, c)
+        for t in range(4):
+            widen(1, t, True, 0)
+        widen(1, 0, True, 1)
         inter_eff(1, True, 0)
-        inter_eff(1, False, 1)
-        invert_var()
-        root_var()
+        widen(1, 1, True, 1)
+        widen(1, 2, False, 1)
+        widen(1, 3, False, 1)
         quant_eff(1, 0)
+        inter_eff(1, True, 1, 0, HALF // 2)
+        inter_eff(1, False, 1, HALF // 2, HALF)
         quant_pred(2, 0)
         quant_eff(1, 1)
-        quant_pred(2, 1)
-        sort(3, 0)
-        sort(3, 1)
-        for h in range(2):
-            for g in range(2):
-                for i, (a, c) in enumerate(pairs):
-                    fit_pair(g, a, c, h, (4 + 4 * g + i) % 8)
-        for a, c in pairs:
-            resid_pair(0, a, c)
         for t in range(4):
-            turn_sorted(3, t, 4 + t)
-        for a, c in pairs:
-            resid_pair(1, a, c)
+            sort_slot(3, t)
+        home = {(g, a, c): (4 + 4 * g + 2 * c + a) % 8 for g in range(2) for a in range(2) for c in range(2)}
+        for g in range(2):
+            for c in range(2):
+                for a in range(2):
+                    fit_pair(g, a, c, 0, home[g, a, c])
+        for c in range(2):
+            for g in range(2):
+                for a in range(2):
+                    fit_pair(g, a, c, 1, home[g, a, c])
+        for g in range(2):
+            for a in range(2):
+                resid_pair(g, a, 0)
+        first_free = (4, 5, 0, 1)
+        second_free = (6, 7, 2, 3)
+        for t in range(4):
+            turn_sorted(3, t, first_free[t])
+        quant_pred(2, 1)
+        resid_pair(0, 0, 1)
+        resid_pair(0, 1, 1)
         for t in range(4):
             take(3, t)
-        for i, (a, c) in enumerate(pairs):
+        by_slots = [(0, 0), (0, 1), (1, 0), (1, 1)]
+        for i, (a, c) in enumerate(by_slots):
             for h in range(2):
-                fit_pair(2, a, c, h, i)
+                fit_pair(2, a, c, h, first_free[i])
         weave(0, 0)
         weave(0, 1)
         weave(1, 0)
-        weave(1, 1)
         quant_pred(3, 0)
+        resid_pair(1, 0, 1)
         quant_pred(3, 1)
-        for i, (a, c) in enumerate([(0, 0), (0, 1), (1, 0), (1, 1)]):
+        resid_pair(1, 1, 1)
+        for i, (a, c) in enumerate(by_slots):
             for h in range(2):
-                fit_pair(3, a, c, h, 4 + i)
+                fit_pair(3, a, c, h, second_free[i])
+        spill_pair(2, 0, 0)
+        weave(1, 1)
+        spill_pair(2, 1, 0)
+        spill_pair(2, 1, 1)
         quant_resid(0, 0)
         quant_resid(0, 1)
-        resid_pair(2, 0, 0)
-        spill_pair(2, 0, 1)
-        spill_pair(2, 1, 1)
+        resid_pair(2, 0, 1)
         quant_resid(1, 0)
         quant_resid(1, 1)
+        resid_pair(2, 0, 0)
         resid_pair(2, 1, 0)
-        resid_pair(2, 0, 1)
         resid_pair(2, 1, 1)
         spill_pair(3, 0, 0)
         weave(2, 0)
-        spill_pair(3, 0, 1)
         weave(2, 1)
+        resid_pair(3, 0, 1)
         resid_pair(3, 1, 0)
         quant_resid(2, 0)
-        resid_pair(3, 1, 1)
         quant_resid(2, 1)
+        resid_pair(3, 1, 1)
         resid_pair(3, 0, 0)
-        resid_pair(3, 0, 1)
-        weave(3, 0)
         weave(3, 1)
-        quant_resid(3, 0)
+        root_var()
+        weave(3, 0, True)
         quant_resid(3, 1)
-        for first, second in ((0, 2), (1, 3)):
+        quant_resid(3, 0)
+        for first, second in ((4, 5), (0, 1)):
             for g in range(2):
                 score(first, g)
                 score(second, g)
-        for v in range(4, 8):
+        for v in second_free[:3]:
             score(v, 0)
             score(v, 1)
-        for v in range(8):
+        for v in first_free + second_free[:3]:
             score(v, 2)
+        for g in range(3):
+            score(second_free[3], g)
         for v in range(8):
             score(v, 3)
             finish(v)

@@ -26,9 +26,10 @@ NV = VARIANTS // P
 HALF = TRAITS // 2
 BANKS = 8
 QUAD = 32
+LAST_WIDTHS = (256, 128, 128)
 RESULT_BUFS = 8
 STAGE_BUFS = 4
-HALVED_FROM = NV - 6
+HALVED_FROM = NV - 7
 
 
 def tile_gwas_score_statistics_s13_kernel(
@@ -283,12 +284,14 @@ def tile_gwas_score_statistics_s13_kernel(
                 store(v, scored[v][:, cols], res[:, cols], cols)
 
         def last_tile(v):
-            for q in range(4):
-                cols = slice(q * P, (q + 1) * P)
-                acc = psum.tile([P, P], F32, name="bank%d" % ((v + q) % BANKS))
+            col = 0
+            for q, width in enumerate(LAST_WIDTHS):
+                cols = slice(col, col + width)
+                col = col + width
+                acc = psum.tile([P, width], F32, name="bank%d" % ((v + q) % BANKS))
                 for g in range(G):
                     score_pass(v, g, acc[:], cols)
-                res = kept([P, P], F32, "last%d" % q)
+                res = kept([P, width], F32, "last%d" % q)
                 store(v, acc[:], res[:], cols)
 
         load_eff(0)
@@ -369,40 +372,47 @@ def tile_gwas_score_statistics_s13_kernel(
         for g in range(2):
             for a in range(2):
                 resid_pair(g, a, 0)
-        first_free = (4, 5, 0, 1)
-        second_free = (6, 7, 2, 3)
-        for t in range(4):
-            turn_sorted(3, t, first_free[t])
-        quant_pred(2, 1)
+        weave(0, 0)
+        turn_sorted(3, 0, 4)
+        turn_sorted(3, 1, 5)
+        for c in range(2):
+            for h in range(2):
+                fit_pair(2, 0, c, h, c)
         resid_pair(0, 0, 1)
         resid_pair(0, 1, 1)
-        for t in range(4):
-            take(3, t)
-        by_slots = [(0, 0), (0, 1), (1, 0), (1, 1)]
-        for i, (a, c) in enumerate(by_slots):
-            for h in range(2):
-                fit_pair(2, a, c, h, first_free[i])
-        weave(0, 0)
-        weave(0, 1)
+        turn_sorted(3, 2, 6)
+        turn_sorted(3, 3, 7)
+        take(3, 0)
+        take(3, 1)
         weave(1, 0)
-        quant_pred(3, 0)
-        resid_pair(1, 0, 1)
-        quant_pred(3, 1)
-        resid_pair(1, 1, 1)
-        for i, (a, c) in enumerate(by_slots):
+        take(3, 2)
+        take(3, 3)
+        weave(0, 1)
+        quant_pred(2, 1)
+        for c in range(2):
             for h in range(2):
-                fit_pair(3, a, c, h, second_free[i])
-        spill_pair(2, 0, 0)
+                fit_pair(2, 1, c, h, 4 + c)
+        resid_pair(1, 0, 1)
+        quant_pred(3, 0)
+        resid_pair(1, 1, 1)
         weave(1, 1)
+        quant_resid(0, 0)
+        quant_pred(3, 1)
+        for c in range(2):
+            for h in range(2):
+                fit_pair(3, 0, c, h, 2 + c)
+        for c in range(2):
+            for h in range(2):
+                fit_pair(3, 1, c, h, 6 + c)
+        spill_pair(2, 0, 1)
         spill_pair(2, 1, 0)
         spill_pair(2, 1, 1)
-        quant_resid(0, 0)
         quant_resid(0, 1)
-        resid_pair(2, 0, 1)
+        resid_pair(2, 0, 0)
         quant_resid(1, 0)
         quant_resid(1, 1)
-        resid_pair(2, 0, 0)
         resid_pair(2, 1, 0)
+        resid_pair(2, 0, 1)
         resid_pair(2, 1, 1)
         spill_pair(3, 0, 0)
         weave(2, 0)
@@ -418,17 +428,17 @@ def tile_gwas_score_statistics_s13_kernel(
         weave(3, 0, True)
         quant_resid(3, 1)
         quant_resid(3, 0)
-        for first, second in ((4, 5), (0, 1)):
+        for first, second in ((1, 0), (4, 5)):
             for g in range(2):
                 score(first, g)
                 score(second, g)
-        for v in second_free[:3]:
+        for v in (2, 3, 6):
             score(v, 0)
             score(v, 1)
-        for v in first_free + second_free[:3]:
+        for v in (1, 0, 4, 5, 2, 3, 6):
             score(v, 2)
         for g in range(3):
-            score(second_free[3], g)
+            score(7, g)
         for v in range(8):
             score(v, 3)
             finish(v)

@@ -27,9 +27,9 @@ HALF = TRAITS // 2
 BANKS = 8
 QUAD = 32
 LAST_WIDTHS = (256, 128, 128)
-RESULT_BUFS = 8
+RESULT_BUFS = 7
 STAGE_BUFS = 4
-HALVED_FROM = NV - 7
+HALVED_FROM = NV - 8
 
 
 def tile_gwas_score_statistics_s13_kernel(
@@ -183,7 +183,7 @@ def tile_gwas_score_statistics_s13_kernel(
                     nc.tensor.transpose(turned[g, t][:, h, u, :], src, ident[:])
 
         def sort_slot(g, t, on_vector=False):
-            p_sorted[g, t] = kept([P, H, 2, P], F32, "p_sorted%d_%d" % (g, t))
+            p_sorted[g, t] = stage.tile([P, H, 2, P], F32, name="p_sorted", align_bytes=256)
             words = p_raw[g, t].bitcast(F32)
             copy(p_sorted[g, t][:], words.rearrange("p (h w u) -> p h u w", u=2, w=P), on_vector)
 
@@ -208,6 +208,14 @@ def tile_gwas_score_statistics_s13_kernel(
                 in_=p_grp[g, a][:].rearrange("p t h r j -> p (t h r j)"),
             )
 
+        def quant_slot(g, t):
+            a, e = divmod(t, 2)
+            nc.vector.quantize_mx(
+                out=p_codes[g, a][:, e, :, :].rearrange("p h r -> p (h r)").bitcast(FP8X4),
+                scales=p_sc[g, a][:, e, :, :].rearrange("p h r -> p (h r)"),
+                in_=p_grp[g, a][:, e, :, :, :].rearrange("p h r j -> p (h r j)"),
+            )
+
         def fit_pair(g, a, c, h, b):
             if h == 0:
                 fitted[g, a, c] = bank(b)
@@ -223,12 +231,12 @@ def tile_gwas_score_statistics_s13_kernel(
                 )
 
         def spill_pair(g, a, c):
-            spilled[g, a, c] = stage.tile([P, HALF, 2], F32, name="spilled", align_bytes=256)
+            spilled[g, a, c] = stage.tile([P, HALF, 2], F32, name="spilled", align_bytes=256, bufs=3)
             nc.scalar.copy(out=spilled[g, a, c][:], in_=fitted[g, a, c][:].rearrange("p (e n) -> p n e", e=2))
 
         def resid_pair(g, a, c):
             if (g, c) not in r_pairs:
-                r_pairs[g, c] = stage.tile([P, 2, HALF, 2], BF16, name="r_pairs", align_bytes=256)
+                r_pairs[g, c] = stage.tile([P, 2, HALF, 2], BF16, name="r_pairs", align_bytes=256, bufs=6)
             if (g, a, c) in spilled:
                 fit_pairs = spilled[g, a, c][:]
             else:
@@ -298,17 +306,16 @@ def tile_gwas_score_statistics_s13_kernel(
         load_pred(0, 0, 2)
         load_pred(0, 2, 4)
         load_pred(1, 0, 2)
-        load_pred(1, 2, 4)
-        load_var()
-        load_pred(2, 0, 2)
-        load_pred(2, 2, 3)
-        load_pred(2, 3, 4)
+        load_pred(1, 2, 3)
+        load_pred(1, 3, 4)
         load_eff(1)
+        load_pred(2, 0, 2)
+        load_pred(2, 2, 4)
+        load_var()
         load_traits(0)
-        load_traits(1)
         load_pred(3, 0, 2)
-        load_pred(3, 2, 3)
-        load_pred(3, 3, 4)
+        load_traits(1)
+        load_pred(3, 2, 4)
         load_traits(2)
         load_scales(0, 0, 2)
         load_words(0, 8, 0, 2)
@@ -334,114 +341,118 @@ def tile_gwas_score_statistics_s13_kernel(
             take(0, t)
         quant_pred(0, 0)
         quant_pred(0, 1)
-        turn_var(3)
-        take(1, 0)
-        take(1, 1)
-        quant_pred(1, 0)
-        invert_var()
         for t in range(4):
-            turn(2, t, t)
-        take(1, 2)
-        take(1, 3)
-        quant_pred(1, 1)
-        for t in range(4):
-            take(2, t)
+            take(1, t)
         for t in range(4):
             widen(1, t, True, 0)
-        widen(1, 0, True, 1)
+        quant_pred(1, 0)
         inter_eff(1, True, 0)
-        widen(1, 1, True, 1)
-        widen(1, 2, False, 1)
-        widen(1, 3, False, 1)
-        quant_eff(1, 0)
-        inter_eff(1, True, 1, 0, HALF // 2)
-        inter_eff(1, False, 1, HALF // 2, HALF)
-        quant_pred(2, 0)
-        quant_eff(1, 1)
         for t in range(4):
-            sort_slot(3, t)
-        home = {(g, a, c): (4 + 4 * g + 2 * c + a) % 8 for g in range(2) for a in range(2) for c in range(2)}
-        for g in range(2):
+            widen(1, t, True, 1)
+        quant_eff(1, 0)
+        inter_eff(1, True, 1)
+        quant_slot(1, 2)
+        quant_eff(1, 1)
+        quant_slot(1, 3)
+        home = {(0, 0, 0): 0, (0, 0, 1): 1, (0, 1, 0): 2, (0, 1, 1): 3, (1, 0, 0): 4, (1, 0, 1): 5}
+        for g, a in ((0, 0), (0, 1), (1, 0)):
             for c in range(2):
-                for a in range(2):
-                    fit_pair(g, a, c, 0, home[g, a, c])
+                fit_pair(g, a, c, 0, home[g, a, c])
+        for t in range(4):
+            sort_slot(2, t)
+        turn_sorted(2, 0, 6)
+        turn_sorted(2, 1, 7)
+        take(2, 0)
+        take(2, 1)
         for c in range(2):
-            for g in range(2):
-                for a in range(2):
-                    fit_pair(g, a, c, 1, home[g, a, c])
-        for g in range(2):
-            for a in range(2):
-                resid_pair(g, a, 0)
-        weave(0, 0)
-        turn_sorted(3, 0, 4)
-        turn_sorted(3, 1, 5)
+            for g, a in ((0, 0), (0, 1), (1, 0)):
+                fit_pair(g, a, c, 1, home[g, a, c])
+        resid_pair(0, 0, 0)
+        turn_sorted(2, 2, 6)
+        turn_sorted(2, 3, 7)
+        sort_slot(3, 0)
+        sort_slot(3, 1)
+        take(2, 2)
+        take(2, 3)
+        resid_pair(0, 1, 0)
+        quant_pred(2, 0)
         for c in range(2):
             for h in range(2):
-                fit_pair(2, 0, c, h, c)
+                fit_pair(1, 1, c, h, 2 * c)
+        resid_pair(1, 0, 0)
         resid_pair(0, 0, 1)
-        resid_pair(0, 1, 1)
-        turn_sorted(3, 2, 6)
-        turn_sorted(3, 3, 7)
+        turn_sorted(3, 0, 4)
+        turn_sorted(3, 1, 1)
+        sort_slot(3, 2)
+        sort_slot(3, 3)
         take(3, 0)
         take(3, 1)
-        weave(1, 0)
-        take(3, 2)
-        take(3, 3)
-        weave(0, 1)
+        resid_pair(0, 1, 1)
         quant_pred(2, 1)
         for c in range(2):
             for h in range(2):
-                fit_pair(2, 1, c, h, 4 + c)
+                fit_pair(2, 0, c, h, 6 + c)
         resid_pair(1, 0, 1)
-        quant_pred(3, 0)
+        turn_sorted(3, 2, 3)
+        turn_sorted(3, 3, 5)
+        weave(0, 0)
+        take(3, 2)
+        take(3, 3)
+        resid_pair(1, 1, 0)
         resid_pair(1, 1, 1)
-        weave(1, 1)
-        quant_resid(0, 0)
-        quant_pred(3, 1)
-        for c in range(2):
+        quant_pred(3, 0)
+        for c, b in enumerate((4, 1)):
             for h in range(2):
-                fit_pair(3, 0, c, h, 2 + c)
-        for c in range(2):
-            for h in range(2):
-                fit_pair(3, 1, c, h, 6 + c)
-        spill_pair(2, 0, 1)
-        spill_pair(2, 1, 0)
-        spill_pair(2, 1, 1)
-        quant_resid(0, 1)
+                fit_pair(2, 1, c, h, b)
+        turn_var(3)
+        weave(0, 1)
         resid_pair(2, 0, 0)
+        quant_slot(3, 2)
+        quant_slot(3, 3)
+        invert_var()
+        quant_resid(0, 0)
+        for c in range(2):
+            for h in range(2):
+                fit_pair(3, 0, c, h, 2 * c)
+        for c, b in enumerate((5, 3)):
+            for h in range(2):
+                fit_pair(3, 1, c, h, b)
+        weave(1, 0)
+        weave(1, 1)
+        spill_pair(2, 1, 1)
+        spill_pair(3, 0, 0)
+        spill_pair(3, 0, 1)
+        quant_resid(0, 1)
+        resid_pair(2, 0, 1)
+        resid_pair(2, 1, 0)
         quant_resid(1, 0)
         quant_resid(1, 1)
-        resid_pair(2, 1, 0)
-        resid_pair(2, 0, 1)
+        resid_pair(3, 1, 0)
+        resid_pair(3, 1, 1)
         resid_pair(2, 1, 1)
-        spill_pair(3, 0, 0)
         weave(2, 0)
         weave(2, 1)
-        resid_pair(3, 0, 1)
-        resid_pair(3, 1, 0)
         quant_resid(2, 0)
-        quant_resid(2, 1)
-        resid_pair(3, 1, 1)
         resid_pair(3, 0, 0)
-        weave(3, 1)
+        quant_resid(2, 1)
+        resid_pair(3, 0, 1)
+        weave(3, 0)
         root_var()
-        weave(3, 0, True)
-        quant_resid(3, 1)
+        weave(3, 1, True)
         quant_resid(3, 0)
-        for first, second in ((1, 0), (4, 5)):
-            for g in range(2):
-                score(first, g)
-                score(second, g)
-        for v in (2, 3, 6):
+        quant_resid(3, 1)
+        for v in (6, 7, 1, 4, 0):
+            score(v, 0)
+        for v in (6, 7, 1, 4, 0):
+            score(v, 1)
+        for v in (2, 5, 3):
             score(v, 0)
             score(v, 1)
-        for v in (1, 0, 4, 5, 2, 3, 6):
-            score(v, 2)
-        for g in range(3):
-            score(7, g)
-        for v in range(8):
-            score(v, 3)
-            finish(v)
+        for g in (2, 3):
+            for v in range(8):
+                score(v, g)
+                if g == 3:
+                    finish(v)
         for v in range(8, NV - 1):
             for g in range(G):
                 score(v, g)

@@ -368,84 +368,85 @@ def tile_gwas_score_statistics_s13_kernel(
             for g, a in ((0, 0), (0, 1), (1, 0)):
                 fit_pair(g, a, c, 1, home[g, a, c])
         resid_pair(0, 0, 0)
+        sort_slot(3, 0)
         turn_sorted(2, 2, 6)
         turn_sorted(2, 3, 7)
-        sort_slot(3, 0)
+        turn_sorted(3, 0, 0)
         sort_slot(3, 1)
         take(2, 2)
         take(2, 3)
+        take(3, 0)
         resid_pair(0, 1, 0)
+        resid_pair(0, 0, 1)
         quant_pred(2, 0)
         for c in range(2):
             for h in range(2):
-                fit_pair(1, 1, c, h, 2 * c)
-        resid_pair(1, 0, 0)
-        resid_pair(0, 0, 1)
-        turn_sorted(3, 0, 4)
-        turn_sorted(3, 1, 1)
-        sort_slot(3, 2)
-        sort_slot(3, 3)
-        take(3, 0)
-        take(3, 1)
+                fit_pair(1, 1, c, h, 2 - c)
         resid_pair(0, 1, 1)
-        quant_pred(2, 1)
+        resid_pair(1, 0, 0)
         for c in range(2):
             for h in range(2):
-                fit_pair(2, 0, c, h, 6 + c)
-        resid_pair(1, 0, 1)
-        turn_sorted(3, 2, 3)
-        turn_sorted(3, 3, 5)
+                fit_pair(2, 0, c, h, 3 + c)
+        sort_slot(3, 2)
+        sort_slot(3, 3)
         weave(0, 0)
+        turn_sorted(3, 1, 6)
+        turn_sorted(3, 2, 7)
+        turn_sorted(3, 3, 0)
+        take(3, 1)
         take(3, 2)
         take(3, 3)
+        resid_pair(1, 0, 1)
+        quant_slot(3, 0)
+        quant_pred(2, 1)
         resid_pair(1, 1, 0)
         resid_pair(1, 1, 1)
-        quant_pred(3, 0)
-        for c, b in enumerate((4, 1)):
+        quant_slot(3, 1)
+        for c, b in enumerate((5, 2)):
             for h in range(2):
                 fit_pair(2, 1, c, h, b)
-        turn_var(3)
-        weave(0, 1)
         resid_pair(2, 0, 0)
         quant_slot(3, 2)
         quant_slot(3, 3)
-        invert_var()
-        quant_resid(0, 0)
-        for c in range(2):
+        for c, b in enumerate((1, 6)):
             for h in range(2):
-                fit_pair(3, 0, c, h, 2 * c)
-        for c, b in enumerate((5, 3)):
+                fit_pair(3, 0, c, h, b)
+            if c == 0:
+                turn_var(7)
+        quant_resid(0, 0)
+        invert_var()
+        for c, b in enumerate((0, 7)):
             for h in range(2):
                 fit_pair(3, 1, c, h, b)
+        weave(0, 1)
+        spill_pair(2, 1, 0)
         weave(1, 0)
         weave(1, 1)
-        spill_pair(2, 1, 1)
         spill_pair(3, 0, 0)
         spill_pair(3, 0, 1)
         quant_resid(0, 1)
         resid_pair(2, 0, 1)
-        resid_pair(2, 1, 0)
+        resid_pair(2, 1, 1)
         quant_resid(1, 0)
         quant_resid(1, 1)
         resid_pair(3, 1, 0)
         resid_pair(3, 1, 1)
-        resid_pair(2, 1, 1)
-        weave(2, 0)
+        resid_pair(2, 1, 0)
         weave(2, 1)
-        quant_resid(2, 0)
-        resid_pair(3, 0, 0)
+        weave(2, 0)
         quant_resid(2, 1)
+        resid_pair(3, 0, 0)
+        quant_resid(2, 0)
         resid_pair(3, 0, 1)
         weave(3, 0)
         root_var()
         weave(3, 1, True)
         quant_resid(3, 0)
         quant_resid(3, 1)
-        for v in (6, 7, 1, 4, 0):
-            score(v, 0)
-        for v in (6, 7, 1, 4, 0):
-            score(v, 1)
-        for v in (2, 5, 3):
+        for g in range(2):
+            for v in (3, 4, 5, 2, 1):
+                score(v, g)
+        for v in (6, 0, 7):
             score(v, 0)
             score(v, 1)
         for g in (2, 3):

@@ -27,7 +27,10 @@ HALF = TRAITS // 2
 BANKS = 8
 QUAD = 32
 LAST_WIDTHS = (256, 128, 128)
-RESULT_BUFS = 7
+RESULT_BUFS = 8
+ALIGN = 256
+QUARTER = 64 * 1024
+SIZES = {F32: 4, I32: 4, U32: 4, BF16: 2, U8: 1}
 STAGE_BUFS = 4
 HALVED_FROM = NV - 8
 
@@ -38,31 +41,39 @@ def tile_gwas_score_statistics_s13_kernel(
     nc = tc.nc
     with ExitStack() as ctx:
         keep = ctx.enter_context(tc.tile_pool(name="keep", bufs=1))
-        work = ctx.enter_context(tc.tile_pool(name="work", bufs=RESULT_BUFS))
-        stage = ctx.enter_context(tc.tile_pool(name="stage", bufs=STAGE_BUFS))
         psum = ctx.enter_context(tc.psum_pool(name="psum", bufs=1))
         ctx.enter_context(tc.manual_schedule())
 
-        def kept(shape, dtype, name):
-            return keep.tile(shape, dtype, name=name, align_bytes=256)
+        fill = [q * QUARTER for q in range(4)]
+        where = {}
+
+        def placed(q, shape, dtype, name, bufs=1):
+            if name not in where:
+                size = SIZES[dtype]
+                for n in shape[1:]:
+                    size = size * n
+                size = -(-size // ALIGN) * ALIGN
+                where[name] = fill[q]
+                fill[q] = fill[q] + size * bufs
+            return keep.tile(shape, dtype, name=name, align_bytes=ALIGN, offset=where[name], bufs=bufs)
 
         def bank(b):
             return psum.tile([P, TRAITS], F32, name="bank%d" % b)
 
-        ident = kept([P, P], F32, "ident")
+        ident = placed(1, [P, P], F32, "ident")
         make_identity(nc, ident[:])
-        ident_b = kept([P, P], BF16, "ident_b")
+        ident_b = placed(1, [P, P], BF16, "ident_b")
         make_identity(nc, ident_b[:])
-        var_rows = kept([P, P], BF16, "var_rows")
+        var_rows = placed(1, [P, P], BF16, "var_rows")
         nc.vector.memset(var_rows[0 : P - NV, :], 0.0)
         scale_parts = tuple((v0, v0 + BANKS) for v0 in range(0, NV, BANKS))
         g_scales = []
         for v0, v1 in scale_parts:
-            gs = kept([P, G, (v1 - v0) * P], U8, "g_scales%d" % v0)
+            gs = placed(1, [P, G, (v1 - v0) * P], U8, "g_scales%d" % v0)
             nc.vector.memset(gs[:].rearrange("p g n -> p (g n)").bitcast(I32), 0)
             g_scales.append(gs)
 
-        e_scale = kept([P, H * PACK], F32, "e_scale")
+        e_scale = placed(1, [P, H * PACK], F32, "e_scale")
         nc.scalar.dma_start(
             out=e_scale[:].rearrange("p (h t) -> p h t", h=H),
             in_=eff_scale.rearrange("(h p t) o -> p h (t o)", p=P, t=PACK),
@@ -74,7 +85,7 @@ def tile_gwas_score_statistics_s13_kernel(
         e_bytes, p_raw, t_raw, g_words = {}, {}, {}, {}
 
         def load_eff(h):
-            e_bytes[h] = kept([P, PACK * TRAITS], U8, "e_bytes%d" % h)
+            e_bytes[h] = placed(1, [P, PACK * TRAITS], U8, "e_bytes%d" % h)
             nc.sync.dma_start(
                 out=e_bytes[h][:],
                 in_=eff_bytes.rearrange("(h p t) n -> h p (t n)", p=P, t=PACK)[h],
@@ -84,19 +95,19 @@ def tile_gwas_score_statistics_s13_kernel(
         traits_v = traits.rearrange("(g p t) n -> g p t n", p=P, t=PACK)
 
         def load_pred(g, t0, t1):
-            raw = kept([P, t1 - t0, PRED], BF16, "p_raw%d_%d" % (g, t0))
+            raw = placed(0, [P, t1 - t0, PRED], BF16, "p_raw%d_%d" % (g, t0))
             nc.sync.dma_start(out=raw[:], in_=pred_v[g, :, t0:t1, :])
             for t in range(t0, t1):
                 p_raw[g, t] = raw[:, t - t0, :]
 
         def load_traits(g):
-            t_raw[g] = kept([P, PACK, TRAITS], BF16, "t_raw%d" % g)
+            t_raw[g] = placed(0 if g < 3 else 2, [P, PACK, TRAITS], BF16, "t_raw%d" % g)
             nc.sync.dma_start(out=t_raw[g][:], in_=traits_v[g])
 
         words_v = geno_words.bitcast(I32).rearrange("g p n -> p g n")
 
         def load_words(v0, v1, g0, g1):
-            words = kept([P, g1 - g0, (v1 - v0) * P // 2], I32, "g_words%d_%d" % (v0, g0))
+            words = placed(3, [P, g1 - g0, (v1 - v0) * P // 2], I32, "g_words%d_%d" % (v0, g0))
             nc.sync.dma_start(out=words[:], in_=words_v[:, g0:g1, v0 * P // 2 : v1 * P // 2])
             for v in range(v0, v1):
                 for g in range(g0, g1):
@@ -116,22 +127,22 @@ def tile_gwas_score_statistics_s13_kernel(
         e_wide, e_grp, e_codes, e_sc = {}, {}, {}, {}
         for h in range(H):
             for c in range(2):
-                e_wide[h, c] = kept([P, PACK, HALF], BF16, "e_wide%d_%d" % (h, c))
-                e_grp[h, c] = kept([P, HALF, PACK], BF16, "e_grp%d_%d" % (h, c))
-                e_codes[h, c] = kept([P, HALF], U32, "e_codes%d_%d" % (h, c))
-                e_sc[h, c] = kept([P, HALF], U8, "e_sc%d_%d" % (h, c))
+                e_wide[h, c] = placed(1, [P, PACK, HALF], BF16, "e_wide%d_%d" % (h, c))
+                e_grp[h, c] = placed(1, [P, HALF, PACK], BF16, "e_grp%d_%d" % (h, c))
+                e_codes[h, c] = placed(2, [P, HALF], U32, "e_codes%d_%d" % (h, c))
+                e_sc[h, c] = placed(0, [P, HALF], U8, "e_sc%d_%d" % (h, c))
         p_sorted, p_grp, p_codes, p_sc = {}, {}, {}, {}
         r_pairs, r_grp, r_codes, r_sc = {}, {}, {}, {}
         for g in range(G):
             for a in range(2):
-                p_codes[g, a] = kept([P, 2, H, P], U32, "p_codes%d_%d" % (g, a))
-                p_sc[g, a] = kept([P, 2, H, P], U8, "p_sc%d_%d" % (g, a))
+                p_codes[g, a] = placed(3, [P, 2, H, P], U32, "p_codes%d_%d" % (g, a))
+                p_sc[g, a] = placed(1, [P, 2, H, P], U8, "p_sc%d_%d" % (g, a))
             for c in range(2):
-                r_grp[g, c] = kept([P, HALF, PACK], BF16, "r_grp%d_%d" % (g, c))
-            r_codes[g] = kept([P, TRAITS], U32, "r_codes%d" % g)
-            r_sc[g] = kept([P, TRAITS], U8, "r_sc%d" % g)
-        rvar = kept([P, NV], F32, "rvar")
-        rstd = kept([P, NV], F32, "rstd")
+                r_grp[g, c] = placed(2, [P, HALF, PACK], BF16, "r_grp%d_%d" % (g, c))
+            r_codes[g] = placed(2, [P, TRAITS], U32, "r_codes%d" % g)
+            r_sc[g] = placed(0, [P, TRAITS], U8, "r_sc%d" % g)
+        rvar = placed(1, [P, NV], F32, "rvar")
+        rstd = placed(1, [P, NV], F32, "rstd")
 
         def copy(dst, src, on_vector):
             if on_vector:
@@ -183,7 +194,7 @@ def tile_gwas_score_statistics_s13_kernel(
                     nc.tensor.transpose(turned[g, t][:, h, u, :], src, ident[:])
 
         def sort_slot(g, t, on_vector=False):
-            p_sorted[g, t] = stage.tile([P, H, 2, P], F32, name="p_sorted", align_bytes=256)
+            p_sorted[g, t] = placed(1, [P, H, 2, P], F32, "p_sorted", STAGE_BUFS)
             words = p_raw[g, t].bitcast(F32)
             copy(p_sorted[g, t][:], words.rearrange("p (h w u) -> p h u w", u=2, w=P), on_vector)
 
@@ -196,7 +207,7 @@ def tile_gwas_score_statistics_s13_kernel(
 
         def take(g, t, on_vector=False):
             if t % 2 == 0:
-                p_grp[g, t // 2] = stage.tile([P, 2, H, P, PACK], BF16, name="p_grp", align_bytes=256)
+                p_grp[g, t // 2] = placed(1, [P, 2, H, P, PACK], BF16, "p_grp", STAGE_BUFS)
             dst = p_grp[g, t // 2][:, t % 2, :, :, :].rearrange("p h r j -> p (h r j)").bitcast(F32)
             dst = dst.rearrange("p (h r u) -> p h r u", h=H, u=2)
             copy(dst, turned[g, t].rearrange("p h u r -> p h r u"), on_vector)
@@ -231,12 +242,12 @@ def tile_gwas_score_statistics_s13_kernel(
                 )
 
         def spill_pair(g, a, c):
-            spilled[g, a, c] = stage.tile([P, HALF, 2], F32, name="spilled", align_bytes=256, bufs=3)
+            spilled[g, a, c] = placed(2, [P, HALF, 2], F32, "spilled", 3)
             nc.scalar.copy(out=spilled[g, a, c][:], in_=fitted[g, a, c][:].rearrange("p (e n) -> p n e", e=2))
 
         def resid_pair(g, a, c):
             if (g, c) not in r_pairs:
-                r_pairs[g, c] = stage.tile([P, 2, HALF, 2], BF16, name="r_pairs", align_bytes=256, bufs=6)
+                r_pairs[g, c] = placed(2, [P, 2, HALF, 2], BF16, "r_pairs", 6)
             if (g, a, c) in spilled:
                 fit_pairs = spilled[g, a, c][:]
             else:
@@ -285,7 +296,7 @@ def tile_gwas_score_statistics_s13_kernel(
             nc.sync.dma_start(out=out[v * P : (v + 1) * P, cols], in_=res)
 
         def finish(v):
-            res = work.tile([P, TRAITS], F32, name="res")
+            res = placed(0, [P, TRAITS], F32, "res", RESULT_BUFS)
             parts = 2 if v >= HALVED_FROM else 1
             for i in range(parts):
                 cols = slice(i * TRAITS // parts, (i + 1) * TRAITS // parts)
@@ -299,7 +310,7 @@ def tile_gwas_score_statistics_s13_kernel(
                 acc = psum.tile([P, width], F32, name="bank%d" % ((v + q) % BANKS))
                 for g in range(G):
                     score_pass(v, g, acc[:], cols)
-                res = kept([P, width], F32, "last%d" % q)
+                res = placed(2, [P, width], F32, "last%d" % q)
                 store(v, acc[:], res[:], cols)
 
         load_eff(0)
@@ -454,8 +465,13 @@ def tile_gwas_score_statistics_s13_kernel(
                 score(v, g)
                 if g == 3:
                     finish(v)
-        for v in range(8, NV - 1):
+        for v in range(8, NV - 2, 2):
             for g in range(G):
                 score(v, g)
+                score(v + 1, g)
             finish(v)
+            finish(v + 1)
+        for g in range(G):
+            score(NV - 2, g)
+        finish(NV - 2)
         last_tile(NV - 1)

@@ -29,6 +29,7 @@ QUAD = 32
 LAST_WIDTHS = (256, 128, 128)
 RESULT_BUFS = 8
 ALIGN = 256
+SHIFTS = (64, 192, 64, 192)
 QUARTER = 64 * 1024
 SIZES = {F32: 4, I32: 4, U32: 4, BF16: 2, U8: 1}
 STAGE_BUFS = 4
@@ -44,23 +45,24 @@ def tile_gwas_score_statistics_s13_kernel(
         psum = ctx.enter_context(tc.psum_pool(name="psum", bufs=1))
         ctx.enter_context(tc.manual_schedule())
 
-        fill = [q * QUARTER for q in range(4)]
+        anchor = keep.tile([P, P], F32, name="ident", align_bytes=ALIGN, offset=QUARTER)
+        fill = [0, QUARTER + 512, 2 * QUARTER, 3 * QUARTER]
         where = {}
 
-        def placed(q, shape, dtype, name, bufs=1):
+        def placed(q, shape, dtype, name, bufs=1, shift=0):
             if name not in where:
                 size = SIZES[dtype]
                 for n in shape[1:]:
                     size = size * n
                 size = -(-size // ALIGN) * ALIGN
-                where[name] = fill[q]
-                fill[q] = fill[q] + size * bufs
-            return keep.tile(shape, dtype, name=name, align_bytes=ALIGN, offset=where[name], bufs=bufs)
+                where[name] = fill[q] + shift
+                fill[q] = fill[q] + size * bufs + (ALIGN if shift else 0)
+            return keep.tile(shape, dtype, name=name, align_bytes=64, offset=where[name], bufs=bufs)
 
         def bank(b):
             return psum.tile([P, TRAITS], F32, name="bank%d" % b)
 
-        ident = placed(1, [P, P], F32, "ident")
+        ident = anchor
         make_identity(nc, ident[:])
         ident_b = placed(1, [P, P], BF16, "ident_b")
         make_identity(nc, ident_b[:])
@@ -101,7 +103,7 @@ def tile_gwas_score_statistics_s13_kernel(
                 p_raw[g, t] = raw[:, t - t0, :]
 
         def load_traits(g):
-            t_raw[g] = placed(0 if g < 3 else 2, [P, PACK, TRAITS], BF16, "t_raw%d" % g)
+            t_raw[g] = placed(0 if g < 2 else 2, [P, PACK, TRAITS], BF16, "t_raw%d" % g)
             nc.sync.dma_start(out=t_raw[g][:], in_=traits_v[g])
 
         words_v = geno_words.bitcast(I32).rearrange("g p n -> p g n")
@@ -130,7 +132,7 @@ def tile_gwas_score_statistics_s13_kernel(
                 e_wide[h, c] = placed(1, [P, PACK, HALF], BF16, "e_wide%d_%d" % (h, c))
                 e_grp[h, c] = placed(1, [P, HALF, PACK], BF16, "e_grp%d_%d" % (h, c))
                 e_codes[h, c] = placed(2, [P, HALF], U32, "e_codes%d_%d" % (h, c))
-                e_sc[h, c] = placed(0, [P, HALF], U8, "e_sc%d_%d" % (h, c))
+                e_sc[h, c] = placed(0, [P, HALF], U8, "e_sc%d_%d" % (h, c), shift=SHIFTS[2 * h + c])
         p_sorted, p_grp, p_codes, p_sc = {}, {}, {}, {}
         r_pairs, r_grp, r_codes, r_sc = {}, {}, {}, {}
         for g in range(G):
@@ -140,7 +142,7 @@ def tile_gwas_score_statistics_s13_kernel(
             for c in range(2):
                 r_grp[g, c] = placed(2, [P, HALF, PACK], BF16, "r_grp%d_%d" % (g, c))
             r_codes[g] = placed(2, [P, TRAITS], U32, "r_codes%d" % g)
-            r_sc[g] = placed(0, [P, TRAITS], U8, "r_sc%d" % g)
+            r_sc[g] = placed(0, [P, TRAITS], U8, "r_sc%d" % g, shift=SHIFTS[g])
         rvar = placed(1, [P, NV], F32, "rvar")
         rstd = placed(1, [P, NV], F32, "rstd")
 

from contextlib import ExitStack

import concourse.mybir as mybir
from concourse.masks import make_identity

INDIV, PRED, VARIANTS, TRAITS = 2048, 1024, 3072, 512
FLOPS = 2 * INDIV * PRED * TRAITS + 2 * INDIV * VARIANTS * TRAITS

F32 = mybir.dt.float32
BF16 = mybir.dt.bfloat16
I32 = mybir.dt.int32
U32 = mybir.dt.uint32
U8 = mybir.dt.uint8
FP8 = mybir.dt.float8_e4m3fn
FP8X4 = mybir.dt.float8_e4m3fn_x4
FP4X4 = mybir.dt.float4_e2m1fn_x4
ACT = mybir.ActivationFunctionType
ALU = mybir.AluOpType

P = 128
PACK = 4
K_PASS = P * PACK
G = INDIV // K_PASS
H = PRED // K_PASS
NV = VARIANTS // P
HALF = TRAITS // 2
BANKS = 8
QUAD = 32
LAST_WIDTHS = (256, 128, 128)
RESULT_BUFS = 8
ALIGN = 256
SHIFTS = (64, 192, 64, 192)
QUARTER = 64 * 1024
SIZES = {F32: 4, I32: 4, U32: 4, BF16: 2, U8: 1}
STAGE_BUFS = 4
HALVED_FROM = NV - 8


def tile_gwas_score_statistics_s13_kernel(
    tc, pred, eff_bytes, eff_scale, traits, geno_words, geno_scales, var, out
):
    nc = tc.nc
    with ExitStack() as ctx:
        keep = ctx.enter_context(tc.tile_pool(name="keep", bufs=1))
        psum = ctx.enter_context(tc.psum_pool(name="psum", bufs=1))
        ctx.enter_context(tc.manual_schedule())

        anchor = keep.tile([P, P], F32, name="ident", align_bytes=ALIGN, offset=QUARTER)
        fill = [0, QUARTER + 512, 2 * QUARTER, 3 * QUARTER]
        where = {}

        def placed(q, shape, dtype, name, bufs=1, shift=0):
            if name not in where:
                size = SIZES[dtype]
                for n in shape[1:]:
                    size = size * n
                size = -(-size // ALIGN) * ALIGN
                where[name] = fill[q] + shift
                fill[q] = fill[q] + size * bufs + (ALIGN if shift else 0)
            return keep.tile(shape, dtype, name=name, align_bytes=64, offset=where[name], bufs=bufs)

        def bank(b):
            return psum.tile([P, TRAITS], F32, name="bank%d" % b)

        ident = anchor
        make_identity(nc, ident[:])
        ident_b = placed(1, [P, P], BF16, "ident_b")
        make_identity(nc, ident_b[:])
        var_rows = placed(1, [P, P], BF16, "var_rows")
        nc.vector.memset(var_rows[0 : P - NV, :], 0.0)
        scale_parts = tuple((v0, v0 + BANKS) for v0 in range(0, NV, BANKS))
        g_scales = []
        for v0, v1 in scale_parts:
            gs = placed(1, [P, G, (v1 - v0) * P], U8, "g_scales%d" % v0)
            nc.vector.memset(gs[:].rearrange("p g n -> p (g n)").bitcast(I32), 0)
            g_scales.append(gs)

        e_scale = placed(1, [P, H * PACK], F32, "e_scale")
        nc.scalar.dma_start(
            out=e_scale[:].rearrange("p (h t) -> p h t", h=H),
            in_=eff_scale.rearrange("(h p t) o -> p h (t o)", p=P, t=PACK),
        )

        def load_var():
            nc.sync.dma_start(out=var_rows[P - NV : P, :], in_=var.rearrange("(j p) -> j p", p=P))

        e_bytes, p_raw, t_raw, g_words = {}, {}, {}, {}

        def load_eff(h):
            e_bytes[h] = placed(1, [P, PACK * TRAITS], U8, "e_bytes%d" % h)
            nc.sync.dma_start(
                out=e_bytes[h][:],
                in_=eff_bytes.rearrange("(h p t) n -> h p (t n)", p=P, t=PACK)[h],
            )

        pred_v = pred.rearrange("(g p t) k -> g p t k", p=P, t=PACK)
        traits_v = traits.rearrange("(g p t) n -> g p t n", p=P, t=PACK)

        def load_pred(g, t0, t1):
            raw = placed(0, [P, t1 - t0, PRED], BF16, "p_raw%d_%d" % (g, t0))
            nc.sync.dma_start(out=raw[:], in_=pred_v[g, :, t0:t1, :])
            for t in range(t0, t1):
                p_raw[g, t] = raw[:, t - t0, :]

        def load_traits(g):
            t_raw[g] = placed(0 if g < 2 else 2, [P, PACK, TRAITS], BF16, "t_raw%d" % g)
            nc.sync.dma_start(out=t_raw[g][:], in_=traits_v[g])

        words_v = geno_words.bitcast(I32).rearrange("g p n -> p g n")

        def load_words(v0, v1, g0, g1):
            words = placed(3, [P, g1 - g0, (v1 - v0) * P // 2], I32, "g_words%d_%d" % (v0, g0))
            nc.sync.dma_start(out=words[:], in_=words_v[:, g0:g1, v0 * P // 2 : v1 * P // 2])
            for v in range(v0, v1):
                for g in range(g0, g1):
                    g_words[v, g] = words[:, g - g0, (v - v0) * P // 2 : (v - v0 + 1) * P // 2]

        scale_rows = geno_scales.bitcast(I32).rearrange("g (q r) n -> r q g n", r=4)

        def load_scales(part, g0=0, g1=G):
            v0, v1 = scale_parts[part]
            dst = g_scales[part][:].rearrange("p g n -> p (g n)").bitcast(I32)
            dst = dst.rearrange("p (g n) -> p g n", g=G)
            for r in range(4):
                nc.sync.dma_start(
                    out=dst[r:P:QUAD, g0:g1, :], in_=scale_rows[r][:, g0:g1, v0 * P // 4 : v1 * P // 4]
                )

        e_wide, e_grp, e_codes, e_sc = {}, {}, {}, {}
        for h in range(H):
            for c in range(2):
                e_wide[h, c] = placed(1, [P, PACK, HALF], BF16, "e_wide%d_%d" % (h, c))
                e_grp[h, c] = placed(1, [P, HALF, PACK], BF16, "e_grp%d_%d" % (h, c))
                e_codes[h, c] = placed(2, [P, HALF], U32, "e_codes%d_%d" % (h, c))
                e_sc[h, c] = placed(0, [P, HALF], U8, "e_sc%d_%d" % (h, c), shift=SHIFTS[2 * h + c])
        p_sorted, p_grp, p_codes, p_sc = {}, {}, {}, {}
        r_pairs, r_grp, r_codes, r_sc = {}, {}, {}, {}
        for g in range(G):
            for a in range(2):
                p_codes[g, a] = placed(3, [P, 2, H, P], U32, "p_codes%d_%d" % (g, a))
                p_sc[g, a] = placed(1, [P, 2, H, P], U8, "p_sc%d_%d" % (g, a))
            for c in range(2):
                r_grp[g, c] = placed(2, [P, HALF, PACK], BF16, "r_grp%d_%d" % (g, c))
            r_codes[g] = placed(2, [P, TRAITS], U32, "r_codes%d" % g)
            r_sc[g] = placed(0, [P, TRAITS], U8, "r_sc%d" % g, shift=SHIFTS[g])
        rvar = placed(1, [P, NV], F32, "rvar")
        rstd = placed(1, [P, NV], F32, "rstd")

        def copy(dst, src, on_vector):
            if on_vector:
                nc.vector.tensor_copy(out=dst, in_=src)
            else:
                nc.scalar.copy(out=dst, in_=src)

        turned, fitted, spilled, scored = {}, {}, {}, {}

        def turn_var(b):
            turned["var"] = psum.tile([P, P], F32, name="bank%d" % b)
            nc.tensor.matmul(turned["var"][:], lhsT=var_rows[:], rhs=ident_b[:], start=True, stop=True)

        def invert_var():
            nc.vector.reciprocal(out=rvar[:], in_=turned["var"][:, P - NV : P])

        def root_var():
            nc.scalar.activation(out=rstd[:], in_=rvar[:], func=ACT.Sqrt)

        def widen(h, t, on_vector, c):
            col = t * TRAITS + c * HALF
            raw = e_bytes[h][:, col : col + HALF].bitcast(FP8)
            scale = e_scale[:, h * PACK + t : h * PACK + t + 1]
            if on_vector:
                nc.vector.tensor_scalar(
                    out=e_wide[h, c][:, t, :], in0=raw, scalar1=scale, scalar2=None, op0=ALU.mult
                )
            else:
                nc.scalar.activation(out=e_wide[h, c][:, t, :], in_=raw, func=ACT.Copy, scale=scale)

        def inter_eff(h, on_vector, c, lo=0, hi=HALF):
            dst = e_grp[h, c][:, lo:hi, :].rearrange("p (n i) t -> p n t i", i=4)
            src = e_wide[h, c][:, :, lo:hi].rearrange("p t (n i) -> p n t i", i=4)
            copy(dst, src, on_vector)

        def quant_eff(h, c):
            nc.vector.quantize_mx(
                out=e_codes[h, c][:].bitcast(FP8X4),
                scales=e_sc[h, c][:],
                in_=e_grp[h, c][:].rearrange("p n t -> p (n t)"),
            )

        def turn(g, t, b):
            turned[g, t] = bank(b)[:].rearrange("p (h u r) -> p h u r", h=H, u=2)
            words = p_raw[g, t].bitcast(F32)
            for h in range(H):
                for u in range(2):
                    src = words[:, 256 * h + u : 256 * (h + 1) : 2]
                    nc.tensor.transpose(turned[g, t][:, h, u, :], src, ident[:])

        def sort_slot(g, t, on_vector=False):
            p_sorted[g, t] = placed(1, [P, H, 2, P], F32, "p_sorted", STAGE_BUFS)
            words = p_raw[g, t].bitcast(F32)
            copy(p_sorted[g, t][:], words.rearrange("p (h w u) -> p h u w", u=2, w=P), on_vector)

        def turn_sorted(g, t, b):
            turned[g, t] = bank(b)[:].rearrange("p (h u r) -> p h u r", h=H, u=2)
            for h in range(H):
                for u in range(2):
                    src = p_sorted[g, t][:, h, u, :]
                    nc.tensor.transpose(turned[g, t][:, h, u, :], src, ident[:])

        def take(g, t, on_vector=False):
            if t % 2 == 0:
                p_grp[g, t // 2] = placed(1, [P, 2, H, P, PACK], BF16, "p_grp", STAGE_BUFS)
            dst = p_grp[g, t // 2][:, t % 2, :, :, :].rearrange("p h r j -> p (h r j)").bitcast(F32)
            dst = dst.rearrange("p (h r u) -> p h r u", h=H, u=2)
            copy(dst, turned[g, t].rearrange("p h u r -> p h r u"), on_vector)

        def quant_pred(g, a):
            nc.vector.quantize_mx(
                out=p_codes[g, a][:].rearrange("p t h r -> p (t h r)").bitcast(FP8X4),
                scales=p_sc[g, a][:].rearrange("p t h r -> p (t h r)"),
                in_=p_grp[g, a][:].rearrange("p t h r j -> p (t h r j)"),
            )

        def quant_slot(g, t):
            a, e = divmod(t, 2)
            nc.vector.quantize_mx(
                out=p_codes[g, a][:, e, :, :].rearrange("p h r -> p (h r)").bitcast(FP8X4),
                scales=p_sc[g, a][:, e, :, :].rearrange("p h r -> p (h r)"),
                in_=p_grp[g, a][:, e, :, :, :].rearrange("p h r j -> p (h r j)"),
            )

        def fit_pair(g, a, c, h, b):
            if h == 0:
                fitted[g, a, c] = bank(b)
            for e in range(2):
                nc.tensor.matmul_mx(
                    out=fitted[g, a, c][:, e * HALF : (e + 1) * HALF],
                    lhsT=p_codes[g, a][:, e, h, :].bitcast(FP8X4),
                    lhsT_scale=p_sc[g, a][:, e, h, :],
                    rhs=e_codes[h, c][:].bitcast(FP8X4),
                    rhs_scale=e_sc[h, c][:],
                    start=(h == 0 and e == 0),
                    stop=(h == H - 1 and e == 1),
                )

        def spill_pair(g, a, c):
            spilled[g, a, c] = placed(2, [P, HALF, 2], F32, "spilled", 3)
            nc.scalar.copy(out=spilled[g, a, c][:], in_=fitted[g, a, c][:].rearrange("p (e n) -> p n e", e=2))

        def resid_pair(g, a, c):
            if (g, c) not in r_pairs:
                r_pairs[g, c] = placed(2, [P, 2, HALF, 2], BF16, "r_pairs", 6)
            if (g, a, c) in spilled:
                fit_pairs = spilled[g, a, c][:]
            else:
                fit_pairs = fitted[g, a, c][:].rearrange("p (e n) -> p n e", e=2)
            rows = t_raw[g][:, 2 * a : 2 * a + 2, c * HALF : (c + 1) * HALF]
            nc.vector.tensor_tensor(
                out=r_pairs[g, c][:, a, :, :],
                in0=rows.rearrange("p e n -> p n e"),
                in1=fit_pairs,
                op=ALU.subtract,
            )

        def weave(g, c, on_vector=False):
            dst = r_grp[g, c][:].rearrange("p n t -> p (n t)").bitcast(F32)
            src = r_pairs[g, c][:].rearrange("p a n e -> p (a n e)").bitcast(F32)
            copy(dst.rearrange("p (n a) -> p n a", a=2), src.rearrange("p (a n) -> p n a", a=2), on_vector)

        def quant_resid(g, c):
            cols = slice(c * HALF, (c + 1) * HALF)
            nc.vector.quantize_mx(
                out=r_codes[g][:, cols].bitcast(FP8X4),
                scales=r_sc[g][:, cols],
                in_=r_grp[g, c][:].rearrange("p n t -> p (n t)"),
            )

        def score_pass(v, g, acc, cols):
            part = v // BANKS
            col = (v - scale_parts[part][0]) * P
            nc.tensor.matmul_mx(
                out=acc,
                lhsT=g_words[v, g].bitcast(FP4X4),
                lhsT_scale=g_scales[part][:, g, col : col + P],
                rhs=r_codes[g][:, cols].bitcast(FP8X4),
                rhs_scale=r_sc[g][:, cols],
                start=(g == 0),
                stop=(g == G - 1),
            )

        def score(v, g):
            if g == 0:
                scored[v] = bank(v % BANKS)
            score_pass(v, g, scored[v][:], slice(0, TRAITS))

        def store(v, acc, res, cols):
            nc.scalar.activation(out=res, in_=acc, func=ACT.Square, scale=rstd[:, v : v + 1])
            nc.sync.dma_start(out=out[v * P : (v + 1) * P, cols], in_=res)

        def finish(v):
            res = placed(0, [P, TRAITS], F32, "res", RESULT_BUFS)
            parts = 2 if v >= HALVED_FROM else 1
            for i in range(parts):
                cols = slice(i * TRAITS // parts, (i + 1) * TRAITS // parts)
                store(v, scored[v][:, cols], res[:, cols], cols)

        def last_tile(v):
            col = 0
            for q, width in enumerate(LAST_WIDTHS):
                cols = slice(col, col + width)
                col = col + width
                acc = psum.tile([P, width], F32, name="bank%d" % ((v + q) % BANKS))
                for g in range(G):
                    score_pass(v, g, acc[:], cols)
                res = placed(2, [P, width], F32, "last%d" % q)
                store(v, acc[:], res[:], cols)

        load_eff(0)
        load_pred(0, 0, 2)
        load_pred(0, 2, 4)
        load_pred(1, 0, 2)
        load_pred(1, 2, 3)
        load_pred(1, 3, 4)
        load_eff(1)
        load_pred(2, 0, 2)
        load_pred(2, 2, 4)
        load_var()
        load_traits(0)
        load_pred(3, 0, 2)
        load_traits(1)
        load_pred(3, 2, 4)
        load_traits(2)
        load_scales(0, 0, 2)
        load_words(0, 8, 0, 2)
        load_traits(3)
        load_scales(0, 2, 4)
        load_words(0, 8, 2, 4)
        for part in range(1, 3):
            load_scales(part)
            load_words(8 * part, 8 * part + 4, 0, 4)
            load_words(8 * part + 4, 8 * part + 8, 0, 4)
        for t in range(4):
            turn(0, t, t)
        for t in range(4):
            turn(1, t, 4 + t)
        for c in range(2):
            for t in range(4):
                widen(0, t, True, c)
        for c in range(2):
            inter_eff(0, True, c)
        for c in range(2):
            quant_eff(0, c)
        for t in range(4):
            take(0, t)
        quant_pred(0, 0)
        quant_pred(0, 1)
        for t in range(4):
            take(1, t)
        for t in range(4):
            widen(1, t, True, 0)
        quant_pred(1, 0)
        inter_eff(1, True, 0)
        for t in range(4):
            widen(1, t, True, 1)
        quant_eff(1, 0)
        inter_eff(1, True, 1)
        quant_slot(1, 2)
        quant_eff(1, 1)
        quant_slot(1, 3)
        home = {(0, 0, 0): 0, (0, 0, 1): 1, (0, 1, 0): 2, (0, 1, 1): 3, (1, 0, 0): 4, (1, 0, 1): 5}
        for g, a in ((0, 0), (0, 1), (1, 0)):
            for c in range(2):
                fit_pair(g, a, c, 0, home[g, a, c])
        for t in range(4):
            sort_slot(2, t)
        turn_sorted(2, 0, 6)
        turn_sorted(2, 1, 7)
        take(2, 0)
        take(2, 1)
        for c in range(2):
            for g, a in ((0, 0), (0, 1), (1, 0)):
                fit_pair(g, a, c, 1, home[g, a, c])
        resid_pair(0, 0, 0)
        sort_slot(3, 0)
        turn_sorted(2, 2, 6)
        turn_sorted(2, 3, 7)
        turn_sorted(3, 0, 0)
        sort_slot(3, 1)
        take(2, 2)
        take(2, 3)
        take(3, 0)
        resid_pair(0, 1, 0)
        resid_pair(0, 0, 1)
        quant_pred(2, 0)
        for c in range(2):
            for h in range(2):
                fit_pair(1, 1, c, h, 2 - c)
        resid_pair(0, 1, 1)
        resid_pair(1, 0, 0)
        for c in range(2):
            for h in range(2):
                fit_pair(2, 0, c, h, 3 + c)
        sort_slot(3, 2)
        sort_slot(3, 3)
        weave(0, 0)
        turn_sorted(3, 1, 6)
        turn_sorted(3, 2, 7)
        turn_sorted(3, 3, 0)
        take(3, 1)
        take(3, 2)
        take(3, 3)
        resid_pair(1, 0, 1)
        quant_slot(3, 0)
        quant_pred(2, 1)
        resid_pair(1, 1, 0)
        resid_pair(1, 1, 1)
        quant_slot(3, 1)
        for c, b in enumerate((5, 2)):
            for h in range(2):
                fit_pair(2, 1, c, h, b)
        resid_pair(2, 0, 0)
        quant_slot(3, 2)
        quant_slot(3, 3)
        for c, b in enumerate((1, 6)):
            for h in range(2):
                fit_pair(3, 0, c, h, b)
            if c == 0:
                turn_var(7)
        quant_resid(0, 0)
        invert_var()
        for c, b in enumerate((0, 7)):
            for h in range(2):
                fit_pair(3, 1, c, h, b)
        weave(0, 1)
        spill_pair(2, 1, 0)
        weave(1, 0)
        weave(1, 1)
        spill_pair(3, 0, 0)
        spill_pair(3, 0, 1)
        quant_resid(0, 1)
        resid_pair(2, 0, 1)
        resid_pair(2, 1, 1)
        quant_resid(1, 0)
        quant_resid(1, 1)
        resid_pair(3, 1, 0)
        resid_pair(3, 1, 1)
        resid_pair(2, 1, 0)
        weave(2, 1)
        weave(2, 0)
        quant_resid(2, 1)
        resid_pair(3, 0, 0)
        quant_resid(2, 0)
        resid_pair(3, 0, 1)
        weave(3, 0)
        root_var()
        weave(3, 1, True)
        quant_resid(3, 0)
        quant_resid(3, 1)
        for g in range(2):
            for v in (3, 4, 5, 2, 1):
                score(v, g)
        for v in (6, 0, 7):
            score(v, 0)
            score(v, 1)
        for g in (2, 3):
            for v in range(8):
                score(v, g)
                if g == 3:
                    finish(v)
        for v in range(8, NV - 2, 2):
            for g in range(G):
                score(v, g)
                score(v + 1, g)
            finish(v)
            finish(v + 1)
        for g in range(G):
            score(NV - 2, g)
        finish(NV - 2)
        last_tile(NV - 1)
